import numpy as np, ml_dtypes
CORES = [3,11,19,27,35,43,51,59]
N = 8
import mx_ref
BF = ml_dtypes.bfloat16
def gentries(a):
    return np.ascontiguousarray(a.reshape(8, 16, -1).transpose(0, 2, 1)).reshape(8, -1)
def gtable(e):
    e = np.asarray(e); return np.ascontiguousarray(e.reshape(8, -1, 16).transpose(0, 2, 1)).reshape(128, -1).astype(np.int32)
def gcols(t, e):
    v = np.concatenate([t.reshape(8, 16, -1, 4), np.zeros((8, 16, 1, 4), BF)], axis=2)
    return np.ascontiguousarray(np.stack([v[g][:, e[g]] for g in range(8)])).reshape(128, -1)
def tile(rs):
    return np.stack(rs, axis=2).reshape(128, -1).astype(BF)
def pick(q, e):
    c = np.concatenate([q[0].reshape(128, -1, 4), np.zeros((128, 1, 4), np.uint8)], axis=1); s = np.concatenate([q[1], np.ones((16, 1), np.uint8)], axis=1)
    return (np.ascontiguousarray(c[:, e].reshape(128, -1)), np.ascontiguousarray(s[:, e]))
def join(*qs):
    return (np.concatenate([q[0] for q in qs], axis=1), np.concatenate([q[1] for q in qs], axis=1))
def put(q, e, v):
    c, s = q[0].reshape(128, -1, 4).copy(), q[1].copy(); c[:, e] = v[0].reshape(128, -1, 4); s[:, e] = v[1]
    return (c.reshape(128, -1), s)
def pk(c, s):
    return (np.ascontiguousarray(c), mx_ref.live(s))
def emit(q):
    return q[0], q[1]
def packed(v, rng):
    q = [mx_ref.quantize(np.ascontiguousarray(v[r])) for r in range(N)]
    return np.stack([a for a, b in q]), np.stack([mx_ref.plane(b, rng) for a, b in q])
def values_of_codes():
    e, c = np.zeros((128, 128, 4), np.float32), np.zeros((128, 2, 4), np.uint8)
    e[np.arange(128), np.arange(128), 0] = 1
    c[:127, :, 0] = np.arange(256).reshape(2, 128).T[:127]
    return mx_ref.matmul(mx_ref.quantize(e.reshape(128, 512).astype(BF)), (c.reshape(128, 8), np.full((16, 2), 127, np.uint8))).T.reshape(-1).astype(np.float64)
CODE_VALUE, SCALE_VALUE = values_of_codes(), 2.0 ** (np.arange(256) - 127.0)
def decode(q):
    return (CODE_VALUE[q[0]].reshape(16, 8, -1, 4) * SCALE_VALUE[q[1]][:, None, :, None] + 0.0).reshape(128, -1).astype(np.float32)
def f(rng, *shape):
    return mx_ref.flush((rng.standard_normal(shape, dtype=np.float32) * np.exp2(rng.integers(-2, 3, shape[:-1] + (1,)))).astype(BF))
def wide(rng, *shape, cols=0):
    v = rng.standard_normal(shape, dtype=np.float32) * np.exp2(rng.integers(-12, 13, shape)).astype(np.float32)
    if cols: v *= np.repeat(np.exp2(rng.integers(-cols, cols + 1, shape[:-2] + (1, shape[-1] // 4))) * (rng.random(shape[:-2] + (1, shape[-1] // 4)) > 0.0625), 4, axis=-1).astype(np.float32)
    return mx_ref.flush(v.astype(BF))
C = 320
STEP = [1, 2, 4]
def numbers_of(rng):
    return {"x": np.array(f(rng, N, 128, 4 * C)), "u": np.array(f(rng, N, 128, 512)), "v": np.array(f(rng, N, 128, 512))}
def stored(w):
    return {"wl": np.stack([gtable(w[r]) for r in range(N)])}
def joined(k):
    w = np.zeros_like(k)
    np.put_along_axis(w, k[..., 0::2], k[..., 1::2], axis=-1)
    np.put_along_axis(w, k[..., 1::2], k[..., 0::2], axis=-1)
    return w
def wiring(rng):
    return stored(joined(rng.permuted(np.tile(np.arange(3 * C), (N, 8, 1)), axis=2)))
def edges(rng):
    w = np.zeros((N, 8, 3 * C), np.int64)
    c, i = np.arange(C), np.arange(3 * C)
    for r in range(N):
        a = C + rng.permutation(2 * C)
        k = [i ^ 1, 3 * C - 1 - i, (i + 3 * (C // 2)) % (3 * C), np.concatenate([c + C, c, (c ^ 1) + 2 * C]), np.concatenate([C - 1 - c, c + 2 * C, c + C]),
             joined(np.concatenate([rng.permutation(C), C + rng.permutation(2 * C)])), joined(np.concatenate([np.stack([c, a[:C]], axis=1).reshape(-1), a[C:]])), joined(rng.permutation(3 * C))]
        w[r, rng.permutation(8)] = np.stack(k)
    return stored(w)
def layers(rng):
    return np.array(f(rng, N, 128, 2048)).reshape(N, 8, 16, 4, 8, 16, 4)
def weights(rng, w):
    c, p = packed(np.ascontiguousarray(w).reshape(N, 128, 2048), rng)
    return {"wc": c, "ws": p}
def blank(d):
    u = d["u"].reshape(N, 128, 128, 4)
    u[:, :, 0::16] = 0
    u[:, :, 1::16] = 0
    return u
def setup_inputs(rng):
    return {**numbers_of(rng), **wiring(rng), **weights(rng, layers(rng))}
def setup_inputs_ties(rng):
    d = numbers_of(rng)
    o = rng.permutation(N)
    k = rng.integers(-1, 2, (N, 8, 2, C)).astype(np.float32)
    k[o[1]] = 1
    x = d["x"].reshape(N, 8, 16, C, 4)
    x[:, :, :3] = 0
    x[:, :, :2, :, 0] = k.astype(BF)
    x[:, :, 2, :, 0] = 1.96875 * 2.0 ** 7
    x[:, :, 3] = (np.array([9.0, 11.0, 5.0, 7.0]) * 2.0 ** -9).astype(np.float32).astype(BF)
    a = np.exp2(rng.integers(-3, 4, (1, 8, 1)).astype(np.float32))
    x[:, :, 8:] = 0
    x[:, :, 8, :, 0] = (-1.125 * a).astype(BF)
    x[:, :, 10, :, 0] = (-0.0703125 * a).astype(BF)
    c = np.ones(N, np.float32)
    c[o[0]] = 0
    c[o[2]] = -1
    u = blank(d)
    for h in range(0, 128, 16):
        for i in range(2): u[:, h + i, h + i, 0] = c.astype(BF)
    w = layers(rng)
    w[:, :, 2] = 0
    w[:, :, :, :, :, :4] = 0
    w[:, :, :, :, :, 8:] = 0
    for g in range(8):
        w[:, g, 8, 0, g, 8, 0] = -28.0
        for b in range(4):
            w[:, g, 10, b, g, 9, 0] = -2.0 ** (b - 5)
            w[:, g, 3, b, g, 3, b] = 64.0
    return {"x": x.reshape(N, 128, 4 * C), "u": u.reshape(N, 128, 512), "v": d["v"], **wiring(rng), **weights(rng, w)}
def setup_inputs_near(rng):
    d = numbers_of(rng)
    o = np.zeros(N, np.int64)
    for i, r in enumerate(rng.permutation([r for r in range(N) if r < (r ^ STEP[0])])):
        o[[r, r ^ STEP[0]]] = rng.permutation([0, 3] if i % 2 == 0 else [1, 2])
    x = d["x"].astype(np.float32).reshape(N, 8, 16, C, 4)
    x[:, :, :8] = 0
    u = blank(d)
    at = [0, C - 1, int(rng.integers(C)), int(rng.integers(C))]
    for r in range(N):
        s = rng.integers(-1, 2, (2, 8, C)).astype(np.float32)
        k = 2.0 ** -30 if o[r] in (0, 3) else 1.0
        for i in range(2):
            if o[r] == 2: x[r, :, 2 * i, :, 0] = s[i] * 2.0 ** -8
            else:
                x[r, :, 2 * i, :, 0] = 1.125 * k * s[i]
                x[r, :, 2 * i + 1, :, 0] = -1.25 * k * s[i]
                for g, j in zip(rng.permutation(8)[:4], at): x[r, g, 2 * i, j, 0] = 2.0 ** 30 * rng.choice([-1.0, 1.0])
            for h in range(0, 128, 16):
                u[r, h + 2 * i, h + i, 0] = 1.125 * k
                u[r, h + 2 * i + 1, h + i, 0] = k
        if o[r] == 2: x[r, :, 4, :, 0] = 1.96875 * 2.0 ** 8
        x[r, :, 5, :, 0] = rng.choice([-1.0, 1.0], (8, C)) * 2.0 ** -30
        x[r, :, 6, :, 0] = 2.0 ** -28
    w = layers(rng)
    w[:, :, :8] = 0
    w[:, :, :, :, :, :8] = 0
    for g in range(8):
        w[:, g, 5, 0, g, 0, 0] = 2.0 ** -8
        w[:, g, 5, 0, g, 2, 0] = 2.0 ** -8
        w[:, g, 5, 0, g, 6, 0] = 32.0
    return {"x": x.reshape(N, 128, 4 * C).astype(BF), "u": u.reshape(N, 128, 512), "v": d["v"], **wiring(rng), **weights(rng, w)}
def setup_inputs_late(rng):
    d = numbers_of(rng)
    c = (rng.permutation(N) % 2 * 2.0 - 1.0).astype(np.float32).astype(BF)
    x = d["x"].reshape(N, 8, 16, C, 4)
    x[:, :, :2] = c[:, None, None, None, None]
    u = blank(d)
    for h in range(0, 128, 16):
        for i in range(2): u[:, h + i, h + i, 0] = 1
    w = layers(rng)
    w[:, :, :, :, :, :2] = (w[:, :, :, :, :, :2].astype(np.float32) * 4).astype(BF)
    return {"x": x.reshape(N, 128, 4 * C), "u": u.reshape(N, 128, 512), "v": d["v"], **edges(rng), **weights(rng, w)}
def setup_inputs_ends(rng):
    d = numbers_of(rng)
    e = [0, STEP[0], STEP[1], STEP[0] ^ STEP[1]]
    e = e + [STEP[2] ^ i for i in e[:N - 4]]
    n = N // 4
    o = np.zeros(N, np.int64)
    o[np.array(e) ^ int(rng.integers(N))] = np.concatenate([np.full(n, 3), np.full(n, 2), rng.permutation(np.arange(2 * n) % 2)])
    x = np.zeros((N, 128, C, 4))
    u = blank(d).astype(np.float32)
    v = rng.choice([-1.0, 1.0], (N, 128, 512))
    w = np.zeros((N, 128, 4, 128, 4), np.float32)
    p = np.arange(128)
    for r in range(N):
        x[r] = (0.9 + 0.02 * rng.random((128, C, 4))) * 2.0 ** 30
        if o[r] == 0: x[r] *= -1
        if o[r] == 1: x[r] *= (1.0 - 2.0 * (np.arange(C) % 2))[None, :, None]
        if o[r] == 2: x[r] *= rng.choice([-1.0, 1.0], (128, C, 4))
        if o[r] == 3:
            x[r] = (1.0 + 0.125 * rng.integers(0, 8, (128, C, 4))) * 2.0 ** -30 * rng.choice([-1.0, 1.0], (1, C, 1))
            x[r, 0::8, :, 0] = 1.5 * 2.0 ** -29
        for i in range(2):
            h = rng.permutation(8)
            u[r, :, i::16] = np.where(h < 2, 0.0, h % 2 * 2.0 - 1.0)[None, :, None] * (2.0 ** -30 if o[r] == 3 else 2.0 ** 30)
        v[r] *= 2.0 ** 30 if o[r] % 2 == 0 else 2.0 ** -30
        for b in range(4): w[r, p, b, p, b] = [-0.25, -0.25, 2.0 ** -8, 256.0][o[r]]
    return {"x": x.astype(np.float32).reshape(N, 128, 4 * C).astype(BF), "u": u.reshape(N, 128, 512).astype(BF), "v": v.astype(np.float32).astype(BF), **edges(rng), **weights(rng, w.astype(BF))}
def setup_inputs_spread(rng):
    d = setup_inputs(rng)
    d["x"] = wide(rng, N, 128, 4 * C, cols=6)
    return d
def check_inputs(d):
    b = []
    for k in ("x", "u", "v"):
        a = np.abs(d[k].astype(np.float32))
        if not (np.isfinite(a).all() and ((a == 0) | (a >= 2.0 ** -30) & (a <= 2.0 ** 30)).all()): b.append("a value of " + k)
    none, least, most = [emit(mx_ref.quantize(np.full((128, 16), k, np.float32).astype(BF)))[1][0, 0] for k in (0.0, 2.0 ** -8, 2.0 ** 8)]
    for r in range(N):
        e, i = gentries(d["wl"][r]), np.arange(3 * C)
        if not ((e >= 0) & (e < 3 * C)).all(): b.append("an entry of wl")
        elif (e == i).any() or (np.take_along_axis(e, e, axis=1) != i).any(): b.append("wl: ports that aren't wired in pairs")
        if ((d["wc"][r] == 0x7F) | (d["wc"][r] == 0xFF)).any(): b.append("wc: a code that is no number")
        s = mx_ref.live(d["ws"][r])
        if ((s != none) & ((s < least) | (s > most))).any(): b.append("ws: a scale out of range")
    return b
def rewired(w, a, b):
    c, d = np.arange(C), w[:, :C]
    active = d < C
    same = a == np.take_along_axis(a, np.minimum(d, C - 1), axis=1)
    turn, cross, swap = active & same, active & ~same, ~active & b
    to = np.concatenate([np.where(turn | swap, c + C, c),
                         np.where(turn, c + 2 * C, np.where(cross, d + C, np.where(swap, c, c + C))),
                         np.where(turn, c, np.where(cross, d + 2 * C, c + 2 * C))], axis=1)
    new = np.zeros_like(to)
    np.put_along_axis(new, to, np.take_along_axis(to, w, axis=1), axis=1)
    return new
def reference(x, u, v, wl, wc, ws):
    qu = [mx_ref.quantize(u[r]) for r in range(N)]
    lay = [pk(wc[r], ws[r]) for r in range(N)]
    wire = [gentries(wl[r]).astype(np.int64) for r in range(N)]
    now = [x[r] for r in range(N)]
    for step in STEP:
        made = []
        for r in range(N):
            s = mx_ref.matmul(qu[r], mx_ref.quantize(now[r]))
            wire[r] = rewired(wire[r], s[0::16] > 0, s[1::16] > 0)
            one, two = gcols(now[r], wire[r][:, C:2 * C] % C), gcols(now[r], wire[r][:, 2 * C:] % C)
            z = mx_ref.quantize(((one.astype(np.float32) + two.astype(np.float32)) * np.float32(0.5)).astype(BF))
            made.append(mx_ref.quantize(tile([mx_ref.matmul(pick(lay[r], np.arange(128 * b, 128 * b + 128)), z) * np.float32(0.03125) for b in range(4)])))
        for r in range(N):
            p = r ^ step
            m = np.take_along_axis(wire[p], wire[r][:, :C], axis=1) % C
            now[r] = (now[r].astype(np.float32) + gcols(decode(made[p]).astype(BF), m).astype(np.float32)).astype(BF)
    y, ow = np.zeros((N, 128, C), np.float32), np.zeros((N, 8, 3 * C), np.float32)
    oc, osc = np.zeros((N, 128, 4 * C), np.uint8), np.zeros((N, 16, C), np.uint8)
    for r in range(N):
        q = mx_ref.quantize(now[r])
        y[r] = mx_ref.matmul(mx_ref.quantize(v[r]), q)
        ow[r] = wire[r]
        oc[r], osc[r] = emit(q)
    return {"y": y, "ow": ow, "oc": oc, "osc": osc}

@@ -1,0 +1,405 @@
+from concourse.mybir import dt, AluOpType as A, ActivationFunctionType as F
+
+N, C, Q, P = 8, 320, 20, 512
+STEP = [1, 2, 4]
+X4, U8, BF, FP, IN, US = "float8_e4m3fn_x4", "uint8", "bfloat16", "float32", "int32", "uint16"
+SCRATCH = {"ps": ("psum", [128, 4096], FP)}
+for _t, _l in (
+        (X4, "uq 128 pq 256 vq 128 wq 512 eq 512 xq 320 zq 320"),
+        (U8, "us 128 pz 256 vs 128 wp 512 es 512 xs 320 zs 320"),
+        (BF, "xi 1280 xh 1280 ut 512 vt 512 eo 512 et 2048 gt 1280 zt 1280 hp 1280 ht 1280"),
+        (BF, "row 640 ma 640 mb 1280 mf 640 ab 320 sa 320 nb 640 nbs 640 bf 1280 bfs 1280"),
+        (IN, "wi 60 pid 1 pim 1 ui 16 ni 60 li 40 mi 20 mj 20"),
+        (US, "ul 16 wu 60 ld 20 eu 80 lx 80 lu 40 mu 20"),
+        (FP, "pc 4 io_ 1536 ioo 1536 cr 20 cw 20 w 80 f 1536 fo 960 fd 640 fds 640 qa 1280 qas 1280 mg 320 mgs 320 yo 320"),
+        (FP, "act 20 in2 40 tb 20 t0 20 td 40 actd 20 a512 20 tt 80 b1 80 b2 80 kk 80 e 80 l1 80 hh 80 sw 80 g1 80 qv 80 ae 80 r 80"),
+        (FP, "pa 80 ix 80 dp 120 p0 120 n2 40 sv 60 bt 80 m 120 a5 120 d2 60")):
+    _l = _l.split()
+    for _i in range(0, len(_l), 2):
+        SCRATCH[_l[_i]] = ("sbuf", [128, int(_l[_i + 1])], _t)
+for _r in range(3):
+    for _n, _w, _t in (("lw", Q, US), ("la", Q, US), ("hq", C, X4), ("hs", C, U8), ("aq", C, X4), ("as", C, U8)):
+        SCRATCH["%s%d" % (_n, _r)] = ("sbuf", [128, _w], _t)
+POOL = {"v": 44, "s": 24, "t": 20, "g": 14, "y": 20, "d": 8}
+SEMAPHORES = ["%s%d" % (q, i) for q in POOL for i in range(POOL[q])] + ["loc"] + ["al%d" % i for i in range(3)] + ["ah%d" % i for i in range(3)]
+
+
+def recorder(g, T):
+    ops, hist, maps = [], {}, {}
+    queue = {"v": g.vector, "s": g.scalar, "t": g.tensor, "g": g, "y": g.sync, "d": g.scalar}
+
+    def cols(v):
+        name, a, b, s = v
+        if SCRATCH[name][0] == "psum":
+            a, b, s = a // 512, (b + 511) // 512, 1
+        k = (a, b, s)
+        if k not in maps:
+            maps[k] = sum(1 << i for i in range(a, b, s))
+        return maps[k]
+
+    def op(q, fn, rd, wr, sem=None):
+        me, deps = len(ops), set()
+        eng = "s" if q == "d" else q
+        for lst, w in ((rd, False), (wr, True)):
+            for v in lst:
+                m, psum = cols(v), SCRATCH[v[0]][0] == "psum"
+                for o, om, ow, oe in hist.setdefault(v[0], []):
+                    if om & m and (w or ow or (psum and oe != eng)):
+                        deps.add(o)
+        for lst, w in ((rd, False), (wr, True)):
+            for v in lst:
+                m, h = cols(v), hist[v[0]]
+                if w:
+                    h[:] = [x for x in h if x[1] & ~m or x[0] == me]
+                h.append((me, m, w, eng))
+        deps.discard(me)
+        ops.append({"q": q, "eng": eng, "fn": fn, "deps": deps, "sem": sem, "waits": [], "inc": False})
+
+    def emit():
+        known, at = {}, []
+        for o in ops:
+            k = known.get(o["eng"], 0)
+            for d in sorted(o["deps"], reverse=True):
+                if not k >> d & 1:
+                    o["waits"].append(d)
+                    ops[d]["inc"] = True
+                    k |= 1 << d | at[d]
+            at.append(k)
+            known[o["eng"]] = k
+        pool, total = {}, {}
+        for i, o in enumerate(ops):
+            if o["fn"] is None:
+                total[o["sem"][0]] = o["sem"][1]
+                o["at"] = o["sem"]
+                continue
+            dma = o["q"] in "yd"
+            if o["sem"] is None and (o["inc"] or dma):
+                p = pool.setdefault(o["q"], [])
+                for s in p:
+                    if at[i] >> s[1] & 1:
+                        break
+                else:
+                    s = ["%s%d" % (o["q"], len(p)), 0]
+                    p.append(s)
+                s[1] = i
+                total[s[0]] = total.get(s[0], 0) + (16 if dma else 1)
+                o["at"] = (s[0], total[s[0]])
+            qu = queue[o["q"]]
+            for d in sorted(o["waits"]):
+                qu.wait_ge(T.sem[ops[d]["at"][0]], ops[d]["at"][1])
+            ins = o["fn"]()
+            if "at" in o:
+                ins.then_inc(T.sem[o["at"][0]], 16 if dma else 1)
+        for s in sorted(total):
+            g.wait_ge(T.sem[s], total[s])
+
+    return op, emit
+
+
+def rank_program(g, core, T, topo):
+    rank = T.rank_of(core)
+    if rank is None:
+        return
+    op, emit = recorder(g, T)
+
+    def v(name, a=0, b=None, s=1):
+        return (name, a, SCRATCH[name][1][1] if b is None else b, s)
+
+    def ap(w):
+        n, a, b, s = w
+        return T[n][:, a:b] if s == 1 else T[n][:, a:b:s]
+
+    def by(win, off):
+        return ap(win).indirect(ap(off))
+
+    def tt(out, a, b, o):
+        op("v", lambda: g.vector.tensor_tensor(ap(out), ap(a), ap(b), o), [a, b], [out])
+
+    def ttx(out, win, off, b, o):
+        op("v", lambda: g.vector.tensor_tensor(ap(out), by(win, off), ap(b), o), [win, off, b], [out])
+
+    def ts(out, a, s1, o1, s2=None, o2=None):
+        rd = [a] + [s for s in (s1, s2) if isinstance(s, tuple)]
+        k1, k2 = (ap(s) if isinstance(s, tuple) else s for s in (s1, s2))
+        if o2 is None:
+            op("v", lambda: g.vector.tensor_scalar(ap(out), ap(a), k1, None, o1), rd, [out])
+        else:
+            op("v", lambda: g.vector.tensor_scalar(ap(out), ap(a), k1, k2, o1, o2), rd, [out])
+
+    def cp(out, a):
+        op("v", lambda: g.vector.tensor_copy(ap(out), ap(a)), [a], [out])
+
+    def cpx(q, out, win, off):
+        if q == "v":
+            op("v", lambda: g.vector.tensor_copy(ap(out), by(win, off)), [win, off], [out])
+        else:
+            op("s", lambda: g.scalar.activation(ap(out), by(win, off), F.Copy), [win, off], [out])
+
+    def act(out, a, fn, scale=1.0, bias=0.0):
+        op("s", lambda: g.scalar.activation(ap(out), ap(a), fn, bias=bias, scale=scale), [a], [out])
+
+    def scan(out, m, a):
+        op("v", lambda: g.vector.tensor_tensor_scan(ap(out), ap(m), ap(a), 0.0, A.add, A.max), [m, a], [out])
+
+    def quant(q, s, t):
+        op("v", lambda: g.vector.quantize_mx(ap(q), ap(s), ap(t)), [t], [q, s])
+
+    def mm(out, w, ws, x, xs):
+        op("t", lambda: g.tensor.matmul_mx(ap(out), ap(w), ap(ws), ap(x), ap(xs), True, True), [w, ws, x, xs], [out])
+
+    def iota(out, pat, base, cm, small=False):
+        if small:
+            op("g", lambda: g.iota(ap(out), pat, base, cm, allow_small_or_imprecise_dtypes=True), [], [out])
+        else:
+            op("g", lambda: g.iota(ap(out), pat, base, cm), [], [out])
+
+    def load(q, out, src, codes=False):
+        e = g.sync if q == "y" else g.scalar
+        o = T[out][:].bitcast(dt.uint8) if codes else T[out][:]
+        op(q, lambda: e.dma_start(o, src[:]), [], [v(out)])
+
+    def bank(k):
+        return v("ps", 512 * k, 512 * k + C)
+
+    def send(to, dst, src, sem, codes=False):
+        rid, pid, _ = topo.addr(to)
+        o, i = (T[dst][:].bitcast(dt.uint8), T[src][:].bitcast(dt.uint8)) if codes else (T[dst][:], T[src][:])
+        op("g", lambda: g.remote_dma(o, i, T.sem[sem], T.sem["loc"], pid, rid, topo.mask(core, to)), [v(src)], [], sem=("", 0))
+
+    load("y", "wi", T.wl)
+    load("y", "xi", T.x)
+    load("d", "ut", T.u)
+    load("y", "wp", T.ws)
+    load("y", "wq", T.wc, True)
+    load("d", "vt", T.v)
+
+    iota(v("pid"), [[0, 1]], 0, 1)
+    iota(v("cr"), [[16, Q]], 0, 0, True)
+    iota(v("io_", 0, 1344), [[1, 1344]], 0, 0, True)
+    iota(v("row"), [[0, 40], [1, 16]], 0, 0, True)
+    iota(v("ui"), [[1, 2], [16, 8]], 0, 0)
+    op("v", lambda: g.vector.memset(T.eo[:], 1.0), [], [v("eo")])
+    for k in range(2):
+        o = v("f", P * k + C, P * k + P)
+        op("v", lambda o=o: g.vector.memset(ap(o), 0.0), [], [o])
+    for b in range(4):
+        o = v("et", 512 * b, 512 * b + 512)
+        op("g", lambda o=o, b=b: g.affine_select(ap(o), T.eo[:], [[1, 512]], A.is_equal, 0.0, -b, -4), [v("eo")], [o])
+    iota(v("ioo"), [[C, 3], [1, P]], 0, 0, True)
+    ts(v("pim"), v("pid"), 15, A.bitwise_and)
+    pc = [v("pc", i, i + 1) for i in range(4)]
+    cp(pc[0], v("pim"))
+    thr, corr = pc[1], pc[2]
+    ts(thr, pc[0], -2.0, A.mult, 30.25, A.add)
+    ts(corr, pc[0], -2048.0, A.mult, 30720.0, A.add)
+    ts(v("cw"), v("cr"), pc[0], A.add)
+    cp(v("w", 0, 40), v("wi", Q, 60))
+    cp(v("w", 40, 60), v("wi", 0, Q))
+    x, y = v("b1", 0, 60), v("b2", 0, 60)
+    ts(x, v("w", 0, 60), 320.0, A.is_ge)
+    ts(y, v("w", 0, 60), 640.0, A.is_ge)
+    tt(x, x, y, A.add)
+    ts(v("kk", 0, 60), x, 192.0, A.mult)
+    tt(v("wu"), v("w", 0, 60), v("kk", 0, 60), A.add)
+    ts(v("b2", 0, 40), v("b1", 0, 40), -320.0, A.mult)
+    tt(v("lu"), v("w", 0, 40), v("b2", 0, 40), A.add)
+    tt(v("w", 0, 60), v("w", 0, 60), v("kk", 0, 60), A.add)
+    cp(v("w", 60, 80), v("w", 40, 60))
+
+    def halve(b):
+        act(v("xh", C * b, C * b + C), v("xi", b, 1280, 4), F.Copy, 0.5)
+
+    def tables():
+        for k in range(3):
+            j = (40, 0, Q)[k]
+            cpx("s", v("f", P * k, P * k + C), v("io_", 0, 1344), v("wu", j, j + Q))
+
+    inact = v("in2", 0, Q)
+
+    def pre_a():
+        w0 = v("w", 40, 60)
+        ts(v("act"), w0, 320.0, A.is_lt)
+        tt(v("t0"), w0, v("cw"), A.subtract)
+        ts(v("in2"), v("w", 40, 80), 320.0, A.is_ge)
+        tt(v("t0"), v("t0"), v("act"), A.mult)
+        tt(v("td"), v("w", 40, 80), v("w", 0, 40), A.subtract)
+        tt(v("ld"), v("t0"), v("cw"), A.add)
+
+    def pre_a2():
+        tt(v("actd"), v("act"), v("w", 40, 60), A.mult)
+        ts(v("a512"), v("act"), 512.0, A.mult)
+        tt(v("td"), v("td"), v("in2"), A.mult)
+        cp(v("tt", 40, 60), v("w", 0, Q))
+        tt(v("tt", 60, 80), v("w", Q, 40), v("td", Q, 40), A.add)
+
+    def pre_b1():
+        for k in range(2):
+            cpx("sv"[k], v("fd", C * k, C * k + C), v("f", P * k + P, P * k + P + C), v("ld"))
+        cpx("s", v("qa", 640, 960), v("f", 0, C), v("lu", 0, Q))
+
+    def pre_b2():
+        scan(v("fds"), v("mf"), v("fd"))
+        ts(v("tt", 0, 40), v("fds", 15, 640, 16), corr, A.subtract)
+        tt(v("tt", 0, Q), v("tt", 0, Q), v("td", 0, Q), A.add)
+        t = v("tt")
+        ts(v("b1"), t, 512.0, A.is_ge, 512.0, A.mult)
+        ts(v("b2"), t, 1024.0, A.is_ge, 512.0, A.mult)
+        tt(v("kk"), v("b1"), v("b2"), A.add)
+        tt(v("eu"), t, v("kk"), A.subtract)
+        cpx("s", v("qa", 0, 640), v("f", 0, C), v("eu", 0, 40))
+        cpx("v", v("qa", 960, 1280), v("f", 0, C), v("eu", 60, 80))
+        tt(v("e"), t, v("kk"), A.subtract)
+        ts(v("l1"), t, 512.0, A.is_ge)
+        act(v("sw"), v("b1"), F.Copy, -2.0, 512.0)
+        act(v("g1"), v("b2"), F.Copy, -3.0, 512.0)
+        act(v("hh"), v("kk"), F.Copy, 2.0, -1024.0)
+
+    def pre_c1():
+        scan(v("qas", 0, 640), v("mf"), v("qa", 0, 640))
+        scan(v("qas", 640, 1280), v("mf"), v("qa", 640, 1280))
+        ts(v("qv"), v("qas", 15, 1280, 16), corr, A.subtract)
+        ts(v("ae"), v("qv"), 320.0, A.is_lt)
+        ts(v("ix"), v("ae"), -320.0, A.mult, 320.0, A.add)
+        tt(v("lx"), v("ix"), v("e"), A.add)
+
+    def pre_c2():
+        tt(v("r"), v("qv"), v("e"), A.subtract)
+        tt(v("sw"), v("sw"), v("b2"), A.add)
+        tt(v("pa"), v("ae"), v("g1"), A.mult)
+        tt(v("r"), v("r"), v("l1"), A.mult)
+        tt(v("p0", 80, 120), v("pa", 40, 80), v("tt", 40, 80), A.add)
+        tt(v("r"), v("r"), v("hh"), A.add)
+        tt(v("p0", 0, 40), v("pa", 0, 40), v("tt", 0, 40), A.add)
+        tt(v("r"), v("r"), v("ae"), A.mult)
+        tt(v("p0", 40, 60), v("p0", 80, 100), inact, A.mult)
+
+    def pre_c3():
+        tt(v("dp", 80, 120), v("r", 40, 80), v("sw", 40, 80), A.add)
+        tt(v("p0", 40, 60), v("p0", 40, 60), v("actd"), A.add)
+        tt(v("dp", 60, 80), v("dp", 80, 100), inact, A.mult)
+        tt(v("dp", 40, 60), v("dp", 80, 100), inact, A.mult)
+        tt(v("dp", 0, 40), v("r", 0, 40), v("sw", 0, 40), A.add)
+        tt(v("p0", 60, 80), v("p0", 40, 60), v("a512"), A.add)
+
+    tables()
+    pre_a()
+    pre_a2()
+    ts(v("ma"), v("row"), pc[0], A.is_gt)
+    pre_b1()
+    act(v("mf"), v("ma"), F.Copy, 67584.0, -65536.0)
+    for k in range(2):
+        act(v("mb", 640 * k, 640 * k + 640), v("ma"), F.Copy, 66.0, -64.0)
+    quant(v("uq"), v("us"), v("ut"))
+    cp(v("ul"), v("ui"))
+    op("v", lambda: g.vector.tensor_copy(T.pq[:, 0:256].bitcast(dt.uint32), T.uq[:, 0:128].bitcast(dt.uint32).indirect(T.ul[:, 0:16])), [v("uq"), v("ul")], [v("pq")])
+    op("v", lambda: g.vector.tensor_copy(T.pz[:, 0:256], T.us[:, 0:128].indirect(T.ul[:, 0:16])), [v("us"), v("ul")], [v("pz")])
+    quant(v("xq"), v("xs"), v("xi"))
+    pre_b2()
+
+    def signs():
+        mm(bank(0), v("pq", 0, 128), v("pz", 0, 128), v("xq"), v("xs"))
+        mm(bank(1), v("pq", 128, 256), v("pz", 128, 256), v("xq"), v("xs"))
+        act(v("sa"), bank(0), F.Sign, 1.0, -2.0 ** -93)
+        act(v("nb", C, 640), bank(1), F.Sign)
+        if r:
+            pre_c3()
+        ts(v("ab"), bank(0), 0.0, A.is_le, 0.5, A.subtract)
+        ttx(v("nb", 0, C), v("ab"), v("ld"), v("sa"), A.mult)
+
+    for r in range(3):
+        last = r == 2
+        to = T.cores[rank ^ STEP[r]]
+        ins = len(topo.engines(to, core))
+        signs()
+        if r == 0:
+            pre_c1()
+        cpx("s", v("bf", 0, 640), v("nb"), v("lx", 0, 40))
+        cpx("s", v("bf", 960, 1280), v("nb"), v("lx", 60, 80))
+        if r == 0:
+            pre_c2()
+            pre_c3()
+            for b in range(4):
+                halve(b)
+        scan(v("nbs"), v("mb", 0, 640), v("nb"))
+        cpx("v", v("bf", 640, 960), v("nb"), v("lx", 40, 60))
+        ts(v("n2"), v("nbs", 15, 640, 16), thr, A.is_ge)
+        tt(v("tb"), v("n2", Q, 40), inact, A.mult)
+        tt(v("sv", Q, 40), v("n2", 0, Q), inact, A.add)
+        tt(v("sv", 0, Q), v("n2", 0, Q), v("tb"), A.add)
+        tt(v("sv", 40, 60), v("n2", 0, Q), v("tb"), A.add)
+        scan(v("bfs"), v("mb"), v("bf"))
+        ts(v("bt"), v("bfs", 15, 1280, 16), thr, A.is_ge)
+        tt(v("m", 0, 60), v("bt", 0, 60), v("dp", 0, 60), A.mult)
+        tt(v("m", 60, 80), v("bt", 40, 60), v("dp", 60, 80), A.mult)
+        tt(v("m", 80, 120), v("bt", 40, 80), v("dp", 80, 120), A.mult)
+        tt(v("a5"), v("m"), v("p0"), A.add)
+        tt(v("d2"), v("a5", 0, 60), v("a5", 60, 120), A.subtract)
+        tt(v("d2"), v("d2"), v("sv"), A.mult)
+        tt(v("ni"), v("d2"), v("a5", 60, 120), A.add)
+        ts(v("li"), v("ni", 0, 40), 511, A.bitwise_and)
+        cp(v("lw%d" % r), v("ni", 40, 60))
+        cp(v("lu"), v("li"))
+        send(to, "la%d" % r, "lw%d" % r, "al%d" % r)
+        op("x", None, [], [v("la%d" % r)], sem=("al%d" % r, ins))
+        for t in range(4):
+            cpx("sssv"[t], v("gt", C * t, C * t + C), v("xh", C * t, C * t + C), v("lu", 0, Q))
+        cp(v("wu"), v("ni"))
+        for t in range(4):
+            ttx(v("zt", t, 1280, 4), v("xh", C * t, C * t + C), v("lu", Q, 40), v("gt", C * t, C * t + C), A.add)
+        quant(v("zq"), v("zs"), v("zt"))
+        if not last:
+            cp(v("w", 0, 60), v("ni"))
+            cp(v("w", 60, 80), v("ni", 40, 60))
+        for b in range(4):
+            k = (128 * b, 128 * b + 128)
+            mm(bank(b), v("wq", *k), v("wp", *k), v("zq"), v("zs"))
+        tables()
+        if r == 0:
+            for b in range(4):
+                quant(v("eq", 128 * b, 128 * b + 128), v("es", 128 * b, 128 * b + 128), v("et", 512 * b, 512 * b + 512))
+        if not last:
+            pre_a()
+        hp = [v("hp", C * b, C * b + C) for b in range(4)]
+        cpx("v", v("mg"), v("f", 0, 1344), v("la%d" % r))
+        for b in (0, 1, 2):
+            act(hp[b], bank(b), F.Copy, 0.03125)
+        scan(v("mgs"), v("mf", 0, C), v("mg"))
+        ts(v("mi"), v("mgs", 15, C, 16), corr, A.subtract)
+        ts(v("mj"), v("mi"), 511, A.bitwise_and)
+        cp(v("mu"), v("mj"))
+        ts(hp[3], bank(3), 0.03125, A.mult)
+        for t in (0, 3, 1, 2):
+            cpx("s" if t < 2 else "v", v("ht", t, 1280, 4), hp[t], v("mu"))
+        quant(v("hq%d" % r), v("hs%d" % r), v("ht"))
+        send(to, "aq%d" % r, "hq%d" % r, "ah%d" % r, True)
+        send(to, "as%d" % r, "hs%d" % r, "ah%d" % r)
+        op("x", None, [], [v("aq%d" % r), v("as%d" % r)], sem=("ah%d" % r, 2 * ins))
+        if last:
+            cpx("s", v("fo", 0, C), v("ioo"), v("wu", 40, 60))
+            cpx("s", v("fo", C, 960), v("ioo"), v("wu", 0, 40))
+            op("y", lambda: g.sync.dma_start(T.ow[:], T.fo[0:128:16, 0:960]), [v("fo")], [])
+            quant(v("vq"), v("vs"), v("vt"))
+        else:
+            pre_b1()
+            pre_a2()
+            pre_b2()
+            pre_c1()
+            pre_c2()
+        for b in range(4):
+            k = (128 * b, 128 * b + 128)
+            mm(bank(4 + b), v("eq", *k), v("es", *k), v("aq%d" % r), v("as%d" % r))
+        for b in range(4):
+            x = v("xi", b, 1280, 4)
+            tt(x, bank(4 + b), x, A.add)
+            if not last:
+                halve(b)
+        quant(v("xq"), v("xs"), v("xi"))
+    op("y", lambda: g.sync.dma_start(T.oc[:], T.xq[:].bitcast(dt.uint8)), [v("xq")], [])
+    for k in range(4):
+        op("y" if k % 2 else "d", lambda k=k: (g.sync if k % 2 else g.scalar).dma_start(T.osc[4 * k:4 * k + 4, :], T.xs[32 * k:32 * k + 4, :]), [v("xs")], [])
+    mm(bank(2), v("vq"), v("vs"), v("xq"), v("xs"))
+    cp(v("yo"), bank(2))
+    op("y", lambda: g.sync.dma_start(T.y[:], T.yo[:]), [v("yo")], [])
+
+    emit()
+    g.wait_ge(T.sem["loc"], sum(3 * len(topo.engines(core, T.cores[rank ^ s])) for s in STEP))

@@ -9,16 +9,18 @@ for _t, _l in (
         (U8, "us 128 pz 256 vs 128 wp 512 es 512 xs 320 zs 320"),
         (BF, "xi 1280 xh 1280 ut 512 vt 512 eo 512 et 2048 gt 1280 zt 1280 hp 1280 ht 1280"),
         (BF, "row 640 ma 640 mb 1280 mf 640 ab 320 sa 320 nb 640 nbs 640 bf 1280 bfs 1280"),
-        (IN, "wi 60 pid 1 pim 1 ui 16 ni 60 li 40 mi 20 mj 20"),
-        (US, "ul 16 wu 60 ld 20 eu 80 lx 80 lu 40 mu 20"),
-        (FP, "pc 4 io_ 1536 ioo 1536 cr 20 cw 20 w 80 f 1536 fo 960 fd 640 fds 640 qa 1280 qas 1280 mg 320 mgs 320 yo 320"),
-        (FP, "act 20 in2 40 tb 20 t0 20 td 40 actd 20 a512 20 tt 80 b1 80 b2 80 kk 80 e 80 l1 80 hh 80 sw 80 g1 80 qv 80 ae 80 r 80"),
+        (IN, "wi 60 pid 1 pim 1 ui 16 li 40 mi 20 mj 20 tt 100 ei 80"),
+        (US, "ul 16 ld 20 ldx 20 eu 80 lx 80 lu 40 mu 20"),
+        (FP, "pc 4 io_ 1536 ioo 1536 cr 20 cw 20 b1 60 b2 60 f 1536 fo 960 fd 640 fds 640 qa 1280 qas 1280 mg 320 mgs 320 yo 320"),
+        (FP, "act 20 inn 20 tb 20 t0 20 t1 20 t4 20 inw 20 actd 20 a512 20 kk 80 c1 80 hh 80 sw 80 g1 80 ae 80 r 80"),
         (FP, "pa 80 ix 80 dp 120 p0 120 n2 40 sv 60 bt 80 m 120 a5 120 d2 60")):
     _l = _l.split()
     for _i in range(0, len(_l), 2):
         SCRATCH[_l[_i]] = ("sbuf", [128, int(_l[_i + 1])], _t)
+for _r in range(4):
+    SCRATCH["wu%d" % _r] = ("sbuf", [128, 60], US)
 for _r in range(3):
-    for _n, _w, _t in (("lw", Q, US), ("la", Q, US), ("hq", C, X4), ("hs", C, U8), ("aq", C, X4), ("as", C, U8)):
+    for _n, _w, _t in (("la", Q, US), ("hq", C, X4), ("hs", C, U8), ("aq", C, X4), ("as", C, U8)):
         SCRATCH["%s%d" % (_n, _r)] = ("sbuf", [128, _w], _t)
 POOL = {"v": 44, "s": 24, "t": 20, "g": 14, "y": 20, "d": 8}
 SEMAPHORES = ["%s%d" % (q, i) for q in POOL for i in range(POOL[q])] + ["loc"] + ["al%d" % i for i in range(3)] + ["ah%d" % i for i in range(3)]
@@ -136,7 +138,10 @@ def rank_program(g, core, T, topo):
             op("s", lambda: g.scalar.activation(ap(out), by(win, off), F.Copy), [win, off], [out])
 
     def act(out, a, fn, scale=1.0, bias=0.0):
-        op("s", lambda: g.scalar.activation(ap(out), ap(a), fn, bias=bias, scale=scale), [a], [out])
+        if isinstance(bias, tuple):
+            op("s", lambda: g.scalar.activation(ap(out), ap(a), fn, bias=ap(bias), scale=scale), [a, bias], [out])
+        else:
+            op("s", lambda: g.scalar.activation(ap(out), ap(a), fn, bias=bias, scale=scale), [a], [out])
 
     def scan(out, m, a):
         op("v", lambda: g.vector.tensor_tensor_scan(ap(out), ap(m), ap(a), 0.0, A.add, A.max), [m, a], [out])
@@ -163,10 +168,11 @@ def rank_program(g, core, T, topo):
 
     def send(to, dst, src, sem, codes=False):
         rid, pid, _ = topo.addr(to)
-        o, i = (T[dst][:].bitcast(dt.uint8), T[src][:].bitcast(dt.uint8)) if codes else (T[dst][:], T[src][:])
-        op("g", lambda: g.remote_dma(o, i, T.sem[sem], T.sem["loc"], pid, rid, topo.mask(core, to)), [v(src)], [], sem=("", 0))
+        o, i = (ap(dst).bitcast(dt.uint8), ap(src).bitcast(dt.uint8)) if codes else (ap(dst), ap(src))
+        op("g", lambda: g.remote_dma(o, i, T.sem[sem], T.sem["loc"], pid, rid, topo.mask(core, to)), [src], [], sem=("", 0))
 
-    load("y", "wi", T.wl)
+    op("y", lambda: g.sync.dma_start(T.wi[:, 0:40], T.wl[:, Q:60]), [], [v("wi", 0, 40)])
+    op("d", lambda: g.scalar.dma_start(T.wi[:, 40:60], T.wl[:, 0:Q]), [], [v("wi", 40, 60)])
     load("y", "xi", T.x)
     load("d", "ut", T.u)
     load("y", "wp", T.ws)
@@ -192,85 +198,80 @@ def rank_program(g, core, T, topo):
     thr, corr = pc[1], pc[2]
     ts(thr, pc[0], -2.0, A.mult, 30.25, A.add)
     ts(corr, pc[0], -2048.0, A.mult, 30720.0, A.add)
+    ts(pc[3], pc[0], 2048.0, A.mult, -31744.0, A.add)
     ts(v("cw"), v("cr"), pc[0], A.add)
-    cp(v("w", 0, 40), v("wi", Q, 60))
-    cp(v("w", 40, 60), v("wi", 0, Q))
-    x, y = v("b1", 0, 60), v("b2", 0, 60)
-    ts(x, v("w", 0, 60), 320.0, A.is_ge)
-    ts(y, v("w", 0, 60), 640.0, A.is_ge)
-    tt(x, x, y, A.add)
-    ts(v("kk", 0, 60), x, 192.0, A.mult)
-    tt(v("wu"), v("w", 0, 60), v("kk", 0, 60), A.add)
-    ts(v("b2", 0, 40), v("b1", 0, 40), -320.0, A.mult)
-    tt(v("lu"), v("w", 0, 40), v("b2", 0, 40), A.add)
-    tt(v("w", 0, 60), v("w", 0, 60), v("kk", 0, 60), A.add)
-    cp(v("w", 60, 80), v("w", 40, 60))
+    ts(v("b1"), v("wi"), 320.0, A.is_ge, 192.0, A.mult)
+    ts(v("b2"), v("wi"), 640.0, A.is_ge, 192.0, A.mult)
+    tt(v("b1"), v("b1"), v("b2"), A.add)
+    new, w1, w2, w0, t80 = v("tt", 40, 100), v("tt", 40, 60), v("tt", 60, 80), v("tt", 80, 100), v("tt", 0, 80)
+    tt(v("wu0"), v("wi"), v("b1"), A.add)
+    tt(new, v("wi"), v("b1"), A.add)
+    ts(v("li"), v("tt", 40, 80), 511, A.bitwise_and)
+    cp(v("lu"), v("li"))
 
     def halve(b):
         act(v("xh", C * b, C * b + C), v("xi", b, 1280, 4), F.Copy, 0.5)
 
-    def tables():
+    def tables(wu, qs="sss"):
         for k in range(3):
             j = (40, 0, Q)[k]
-            cpx("s", v("f", P * k, P * k + C), v("io_", 0, 1344), v("wu", j, j + Q))
+            cpx(qs[k], v("f", P * k, P * k + C), v("io_", 0, 1344), v(wu, j, j + Q))
 
-    inact = v("in2", 0, Q)
+    inact = v("inn")
 
     def pre_a():
-        w0 = v("w", 40, 60)
         ts(v("act"), w0, 320.0, A.is_lt)
-        tt(v("t0"), w0, v("cw"), A.subtract)
-        ts(v("in2"), v("w", 40, 80), 320.0, A.is_ge)
-        tt(v("t0"), v("t0"), v("act"), A.mult)
-        tt(v("td"), v("w", 40, 80), v("w", 0, 40), A.subtract)
-        tt(v("ld"), v("t0"), v("cw"), A.add)
+        ts(inact, w0, 320.0, A.is_ge)
+        tt(v("actd"), v("act"), w0, A.mult)
+        tt(v("t0"), inact, v("cw"), A.mult)
+        ts(v("a512"), w0, 320.0, A.is_lt, 512.0, A.mult)
+        tt(v("ld"), v("actd"), v("t0"), A.add)
+        tt(v("t1"), v("t0"), v("a512"), A.add)
+        tt(v("ldx"), v("actd"), v("t1"), A.add)
 
     def pre_a2():
-        tt(v("actd"), v("act"), v("w", 40, 60), A.mult)
-        ts(v("a512"), v("act"), 512.0, A.mult)
-        tt(v("td"), v("td"), v("in2"), A.mult)
-        cp(v("tt", 40, 60), v("w", 0, Q))
-        tt(v("tt", 60, 80), v("w", Q, 40), v("td", Q, 40), A.add)
+        tt(v("t4"), v("act"), w2, A.mult)
+        tt(v("inw"), w0, v("actd"), A.subtract)
+        tt(w2, v("t4"), v("inw"), A.add)
+
+    def pre_b0():
+        cpx("s", v("fd", 0, C), v("f", 0, 1344), v("ldx"))
+        cpx("v", v("fd", C, 640), v("f", 1024, 1344), v("ld"))
 
     def pre_b1():
-        for k in range(2):
-            cpx("sv"[k], v("fd", C * k, C * k + C), v("f", P * k + P, P * k + P + C), v("ld"))
         cpx("s", v("qa", 640, 960), v("f", 0, C), v("lu", 0, Q))
 
     def pre_b2():
         scan(v("fds"), v("mf"), v("fd"))
         ts(v("tt", 0, 40), v("fds", 15, 640, 16), corr, A.subtract)
-        tt(v("tt", 0, Q), v("tt", 0, Q), v("td", 0, Q), A.add)
-        t = v("tt")
-        ts(v("b1"), t, 512.0, A.is_ge, 512.0, A.mult)
-        ts(v("b2"), t, 1024.0, A.is_ge, 512.0, A.mult)
-        tt(v("kk"), v("b1"), v("b2"), A.add)
-        tt(v("eu"), t, v("kk"), A.subtract)
+        ts(v("ei"), t80, 511, A.bitwise_and)
+        cp(v("eu"), v("ei"))
         cpx("s", v("qa", 0, 640), v("f", 0, C), v("eu", 0, 40))
         cpx("v", v("qa", 960, 1280), v("f", 0, C), v("eu", 60, 80))
-        tt(v("e"), t, v("kk"), A.subtract)
-        ts(v("l1"), t, 512.0, A.is_ge)
-        act(v("sw"), v("b1"), F.Copy, -2.0, 512.0)
-        act(v("g1"), v("b2"), F.Copy, -3.0, 512.0)
-        act(v("hh"), v("kk"), F.Copy, 2.0, -1024.0)
+        tt(v("kk"), t80, v("ei"), A.subtract)
 
-    def pre_c1():
-        scan(v("qas", 0, 640), v("mf"), v("qa", 0, 640))
+    def pre_c1(then=None):
+        act(v("hh"), v("kk"), F.Identity, 2.0, pc[3])
+        act(v("g1"), v("kk"), F.Copy, -3.0, 2048.0)
+        act(v("sw"), v("kk"), F.Abs, 2.0, -1280.0)
+        act(v("sw"), v("sw"), F.Copy, 1.0, -768.0)
         scan(v("qas", 640, 1280), v("mf"), v("qa", 640, 1280))
-        ts(v("qv"), v("qas", 15, 1280, 16), corr, A.subtract)
-        ts(v("ae"), v("qv"), 320.0, A.is_lt)
-        ts(v("ix"), v("ae"), -320.0, A.mult, 320.0, A.add)
-        tt(v("lx"), v("ix"), v("e"), A.add)
+        scan(v("qas", 0, 640), v("mf"), v("qa", 0, 640))
+        if then:
+            then()
+        raw = v("qas", 15, 1280, 16)
+        ts(v("ix"), raw, corr, A.subtract, 319.5, A.is_gt)
+        ts(v("ae"), raw, corr, A.subtract, 320.0, A.is_lt)
+        ts(v("ix"), v("ix"), 320.0, A.mult)
+        tt(v("lx"), v("ix"), v("ei"), A.add)
 
     def pre_c2():
-        tt(v("r"), v("qv"), v("e"), A.subtract)
-        tt(v("sw"), v("sw"), v("b2"), A.add)
+        tt(v("c1"), v("hh"), v("ei"), A.subtract)
         tt(v("pa"), v("ae"), v("g1"), A.mult)
-        tt(v("r"), v("r"), v("l1"), A.mult)
+        tt(v("r"), v("qas", 15, 1280, 16), v("c1"), A.add)
         tt(v("p0", 80, 120), v("pa", 40, 80), v("tt", 40, 80), A.add)
-        tt(v("r"), v("r"), v("hh"), A.add)
-        tt(v("p0", 0, 40), v("pa", 0, 40), v("tt", 0, 40), A.add)
         tt(v("r"), v("r"), v("ae"), A.mult)
+        tt(v("p0", 0, 40), v("pa", 0, 40), v("tt", 0, 40), A.add)
         tt(v("p0", 40, 60), v("p0", 80, 100), inact, A.mult)
 
     def pre_c3():
@@ -278,46 +279,48 @@ def rank_program(g, core, T, topo):
         tt(v("p0", 40, 60), v("p0", 40, 60), v("actd"), A.add)
         tt(v("dp", 60, 80), v("dp", 80, 100), inact, A.mult)
         tt(v("dp", 40, 60), v("dp", 80, 100), inact, A.mult)
+
+    def pre_c4():
         tt(v("dp", 0, 40), v("r", 0, 40), v("sw", 0, 40), A.add)
         tt(v("p0", 60, 80), v("p0", 40, 60), v("a512"), A.add)
 
-    tables()
+    tables("wu0", "ssv")
     pre_a()
-    pre_a2()
+    pre_b0()
     ts(v("ma"), v("row"), pc[0], A.is_gt)
-    pre_b1()
     act(v("mf"), v("ma"), F.Copy, 67584.0, -65536.0)
-    for k in range(2):
-        act(v("mb", 640 * k, 640 * k + 640), v("ma"), F.Copy, 66.0, -64.0)
     quant(v("uq"), v("us"), v("ut"))
     cp(v("ul"), v("ui"))
     op("v", lambda: g.vector.tensor_copy(T.pq[:, 0:256].bitcast(dt.uint32), T.uq[:, 0:128].bitcast(dt.uint32).indirect(T.ul[:, 0:16])), [v("uq"), v("ul")], [v("pq")])
-    op("v", lambda: g.vector.tensor_copy(T.pz[:, 0:256], T.us[:, 0:128].indirect(T.ul[:, 0:16])), [v("us"), v("ul")], [v("pz")])
-    quant(v("xq"), v("xs"), v("xi"))
+    pre_a2()
+    pre_b1()
+    op("s", lambda: g.scalar.activation(T.pz[:, 0:256], T.us[:, 0:128].indirect(T.ul[:, 0:16]), F.Copy), [v("us"), v("ul")], [v("pz")])
     pre_b2()
+    act(v("mb", 0, 640), v("ma"), F.Copy, 66.0, -64.0)
+    op("y", lambda: g.sync.dma_start(T.mb[:, 640:1280], T.mb[:, 0:640]), [v("mb", 0, 640)], [v("mb", 640, 1280)])
+    quant(v("xq"), v("xs"), v("xi"))
 
-    def signs():
-        mm(bank(0), v("pq", 0, 128), v("pz", 0, 128), v("xq"), v("xs"))
-        mm(bank(1), v("pq", 128, 256), v("pz", 128, 256), v("xq"), v("xs"))
-        act(v("sa"), bank(0), F.Sign, 1.0, -2.0 ** -93)
-        act(v("nb", C, 640), bank(1), F.Sign)
-        if r:
-            pre_c3()
-        ts(v("ab"), bank(0), 0.0, A.is_le, 0.5, A.subtract)
+    def differ():
+        ts(v("ab"), v("sa"), -0.5, A.mult)
         ttx(v("nb", 0, C), v("ab"), v("ld"), v("sa"), A.mult)
 
     for r in range(3):
         last = r == 2
         to = T.cores[rank ^ STEP[r]]
         ins = len(topo.engines(to, core))
-        signs()
+        wu, la = "wu%d" % (r + 1), v("la%d" % r)
+        mm(bank(0), v("pq", 0, 128), v("pz", 0, 128), v("xq"), v("xs"))
+        mm(bank(1), v("pq", 128, 256), v("pz", 128, 256), v("xq"), v("xs"))
+        act(v("sa"), bank(0), F.Sign, 1.0, -2.0 ** -93)
+        act(v("nb", C, 640), bank(1), F.Sign)
         if r == 0:
-            pre_c1()
+            pre_c1(differ)
+        else:
+            pre_c3()
+            differ()
         cpx("s", v("bf", 0, 640), v("nb"), v("lx", 0, 40))
         cpx("s", v("bf", 960, 1280), v("nb"), v("lx", 60, 80))
         if r == 0:
-            pre_c2()
-            pre_c3()
             for b in range(4):
                 halve(b)
         scan(v("nbs"), v("mb", 0, 640), v("nb"))
@@ -327,7 +330,12 @@ def rank_program(g, core, T, topo):
         tt(v("sv", Q, 40), v("n2", 0, Q), inact, A.add)
         tt(v("sv", 0, Q), v("n2", 0, Q), v("tb"), A.add)
         tt(v("sv", 40, 60), v("n2", 0, Q), v("tb"), A.add)
-        scan(v("bfs"), v("mb"), v("bf"))
+        if r == 0:
+            pre_c2()
+            pre_c3()
+        pre_c4()
+        scan(v("bfs", 0, 960), v("mb", 0, 960), v("bf", 0, 960))
+        scan(v("bfs", 960, 1280), v("mb", 0, C), v("bf", 960, 1280))
         ts(v("bt"), v("bfs", 15, 1280, 16), thr, A.is_ge)
         tt(v("m", 0, 60), v("bt", 0, 60), v("dp", 0, 60), A.mult)
         tt(v("m", 60, 80), v("bt", 40, 60), v("dp", 60, 80), A.mult)
@@ -335,59 +343,55 @@ def rank_program(g, core, T, topo):
         tt(v("a5"), v("m"), v("p0"), A.add)
         tt(v("d2"), v("a5", 0, 60), v("a5", 60, 120), A.subtract)
         tt(v("d2"), v("d2"), v("sv"), A.mult)
-        tt(v("ni"), v("d2"), v("a5", 60, 120), A.add)
-        ts(v("li"), v("ni", 0, 40), 511, A.bitwise_and)
-        cp(v("lw%d" % r), v("ni", 40, 60))
+        tt(new, v("d2"), v("a5", 60, 120), A.add)
+        ts(v("li"), v("tt", 40, 80), 511, A.bitwise_and)
         cp(v("lu"), v("li"))
-        send(to, "la%d" % r, "lw%d" % r, "al%d" % r)
-        op("x", None, [], [v("la%d" % r)], sem=("al%d" % r, ins))
+        cp(v(wu), new)
+        send(to, la, v(wu, 40, 60), "al%d" % r)
+        op("x", None, [], [la], sem=("al%d" % r, ins))
         for t in range(4):
             cpx("sssv"[t], v("gt", C * t, C * t + C), v("xh", C * t, C * t + C), v("lu", 0, Q))
-        cp(v("wu"), v("ni"))
         for t in range(4):
             ttx(v("zt", t, 1280, 4), v("xh", C * t, C * t + C), v("lu", Q, 40), v("gt", C * t, C * t + C), A.add)
         quant(v("zq"), v("zs"), v("zt"))
-        if not last:
-            cp(v("w", 0, 60), v("ni"))
-            cp(v("w", 60, 80), v("ni", 40, 60))
         for b in range(4):
             k = (128 * b, 128 * b + 128)
             mm(bank(b), v("wq", *k), v("wp", *k), v("zq"), v("zs"))
-        tables()
-        if r == 0:
-            for b in range(4):
-                quant(v("eq", 128 * b, 128 * b + 128), v("es", 128 * b, 128 * b + 128), v("et", 512 * b, 512 * b + 512))
+        tables(wu)
         if not last:
             pre_a()
         hp = [v("hp", C * b, C * b + C) for b in range(4)]
-        cpx("v", v("mg"), v("f", 0, 1344), v("la%d" % r))
-        for b in (0, 1, 2):
+        cpx("v", v("mg"), v("f", 0, 1344), la)
+        for b in range(4):
             act(hp[b], bank(b), F.Copy, 0.03125)
         scan(v("mgs"), v("mf", 0, C), v("mg"))
         ts(v("mi"), v("mgs", 15, C, 16), corr, A.subtract)
         ts(v("mj"), v("mi"), 511, A.bitwise_and)
         cp(v("mu"), v("mj"))
-        ts(hp[3], bank(3), 0.03125, A.mult)
         for t in (0, 3, 1, 2):
             cpx("s" if t < 2 else "v", v("ht", t, 1280, 4), hp[t], v("mu"))
-        quant(v("hq%d" % r), v("hs%d" % r), v("ht"))
-        send(to, "aq%d" % r, "hq%d" % r, "ah%d" % r, True)
-        send(to, "as%d" % r, "hs%d" % r, "ah%d" % r)
-        op("x", None, [], [v("aq%d" % r), v("as%d" % r)], sem=("ah%d" % r, 2 * ins))
+        hq, hs, aq, az = (v(n + "%d" % r) for n in ("hq", "hs", "aq", "as"))
+        quant(hq, hs, v("ht"))
+        send(to, aq, hq, "ah%d" % r, True)
+        send(to, az, hs, "ah%d" % r)
+        op("x", None, [], [aq, az], sem=("ah%d" % r, 2 * ins))
         if last:
-            cpx("s", v("fo", 0, C), v("ioo"), v("wu", 40, 60))
-            cpx("s", v("fo", C, 960), v("ioo"), v("wu", 0, 40))
+            cpx("s", v("fo", 0, C), v("ioo"), v(wu, 40, 60))
+            cpx("s", v("fo", C, 960), v("ioo"), v(wu, 0, 40))
             op("y", lambda: g.sync.dma_start(T.ow[:], T.fo[0:128:16, 0:960]), [v("fo")], [])
             quant(v("vq"), v("vs"), v("vt"))
         else:
-            pre_b1()
+            pre_b0()
             pre_a2()
+            pre_b1()
             pre_b2()
+            if r == 0:
+                quant(v("eq"), v("es"), v("et"))
             pre_c1()
             pre_c2()
         for b in range(4):
             k = (128 * b, 128 * b + 128)
-            mm(bank(4 + b), v("eq", *k), v("es", *k), v("aq%d" % r), v("as%d" % r))
+            mm(bank(4 + b), v("eq", *k), v("es", *k), aq, az)
         for b in range(4):
             x = v("xi", b, 1280, 4)
             tt(x, bank(4 + b), x, A.add)

@@ -8,10 +8,10 @@ for _t, _l in (
         (X4, "uq 128 pq 256 vq 128 wq 512 eq 512 xq 320 zq 320"),
         (U8, "us 128 pz 256 vs 128 wp 512 es 512 xs 320 zs 320"),
         (BF, "xi 1280 xh 1280 ut 512 vt 512 eo 512 et 2048 gt 1280 zt 1280 hp 1280 ht 1280"),
-        (BF, "row 640 ma 640 mb 1280 mf 640 ab 320 sa 320 nb 640 nbs 640 bf 1280 bfs 1280"),
+        (BF, "row 320 ma 320 mb 1280 mf 640 ab 320 sa 320 nb 640 nbs 640 bf 1280 bfs 1280"),
         (IN, "wi 60 pid 1 pim 1 ui 16 li 40 mi 20 mj 20 tt 100 ei 80"),
         (US, "ul 16 ld 20 ldx 20 eu 80 lx 80 lu 40 mu 20"),
-        (FP, "pc 4 io_ 1536 ioo 1536 cr 20 cw 20 b1 60 b2 60 f 1536 fo 960 fd 640 fds 640 qa 1280 qas 1280 mg 320 mgs 320 yo 320"),
+        (FP, "pc 5 io_ 1536 ioo 1536 cr 20 cw 20 b1 60 b2 60 f 1536 fo 960 fd 640 fds 640 qa 1280 qas 1280 mg 320 mgs 320 yo 320"),
         (FP, "act 20 inn 20 tb 20 t0 20 t1 20 t4 20 inw 20 actd 20 a512 20 kk 80 c1 80 hh 80 sw 80 g1 80 ae 80 r 80"),
         (FP, "pa 80 ix 80 dp 120 p0 120 n2 40 sv 60 bt 80 m 120 a5 120 d2 60")):
     _l = _l.split()
@@ -23,7 +23,7 @@ for _r in range(3):
     for _n, _w, _t in (("la", Q, US), ("hq", C, X4), ("hs", C, U8), ("aq", C, X4), ("as", C, U8)):
         SCRATCH["%s%d" % (_n, _r)] = ("sbuf", [128, _w], _t)
 POOL = {"v": 44, "s": 24, "t": 20, "g": 14, "y": 20, "d": 8}
-SEMAPHORES = ["%s%d" % (q, i) for q in POOL for i in range(POOL[q])] + ["loc"] + ["al%d" % i for i in range(3)] + ["ah%d" % i for i in range(3)]
+SEMAPHORES = ["%s%d" % (q, i) for q in POOL for i in range(POOL[q])] + ["loc"] + ["al%d" % i for i in range(3)] + ["ah%d" % i for i in range(4)]
 
 
 def recorder(g, T):
@@ -181,25 +181,37 @@ def rank_program(g, core, T, topo):
 
     iota(v("pid"), [[0, 1]], 0, 1)
     iota(v("cr"), [[16, Q]], 0, 0, True)
-    iota(v("io_", 0, 1344), [[1, 1344]], 0, 0, True)
-    iota(v("row"), [[0, 40], [1, 16]], 0, 0, True)
+    iota(v("io_", 0, C), [[1, C]], 0, 0, True)
+    iota(v("row"), [[0, 20], [1, 16]], 0, 0, True)
     iota(v("ui"), [[1, 2], [16, 8]], 0, 0)
     op("v", lambda: g.vector.memset(T.eo[:], 1.0), [], [v("eo")])
     for k in range(2):
-        o = v("f", P * k + C, P * k + P)
-        op("v", lambda o=o: g.vector.memset(ap(o), 0.0), [], [o])
+        for n in ("io_", "f"):
+            o = v(n, P * k + C, P * k + P)
+            op("v", lambda o=o: g.vector.memset(ap(o), 0.0), [], [o])
     for b in range(4):
         o = v("et", 512 * b, 512 * b + 512)
         op("g", lambda o=o, b=b: g.affine_select(ap(o), T.eo[:], [[1, 512]], A.is_equal, 0.0, -b, -4), [v("eo")], [o])
     iota(v("ioo"), [[C, 3], [1, P]], 0, 0, True)
     ts(v("pim"), v("pid"), 15, A.bitwise_and)
-    pc = [v("pc", i, i + 1) for i in range(4)]
+    pc = [v("pc", i, i + 1) for i in range(5)]
     cp(pc[0], v("pim"))
     thr, corr = pc[1], pc[2]
     ts(thr, pc[0], -2.0, A.mult, 30.25, A.add)
     ts(corr, pc[0], -2048.0, A.mult, 30720.0, A.add)
     ts(pc[3], pc[0], 2048.0, A.mult, -31744.0, A.add)
+    ts(pc[4], pc[0], -2048.0, A.mult, 31136.0, A.add)
     ts(v("cw"), v("cr"), pc[0], A.add)
+    for k in (1, 2):
+        act(v("io_", P * k, P * k + C), v("io_", 0, C), F.Copy, 1.0, 1.0 * P * k)
+    ts(v("ma"), v("row"), pc[0], A.is_gt)
+
+    def spread(n, ks):
+        for k in ks:
+            op("y", lambda k=k: g.sync.dma_start(T[n][:, C * k:C * k + C], T[n][:, 0:C]), [v(n, 0, C)], [v(n, C * k, C * k + C)])
+
+    act(v("mf", 0, C), v("ma"), F.Copy, 67584.0, -65536.0)
+    spread("mf", (1,))
     ts(v("b1"), v("wi"), 320.0, A.is_ge, 192.0, A.mult)
     ts(v("b2"), v("wi"), 640.0, A.is_ge, 192.0, A.mult)
     tt(v("b1"), v("b1"), v("b2"), A.add)
@@ -234,9 +246,9 @@ def rank_program(g, core, T, topo):
         tt(v("inw"), w0, v("actd"), A.subtract)
         tt(w2, v("t4"), v("inw"), A.add)
 
-    def pre_b0():
+    def pre_b0(q="s"):
+        cpx(q, v("fd", C, 640), v("f", 1024, 1344), v("ld"))
         cpx("s", v("fd", 0, C), v("f", 0, 1344), v("ldx"))
-        cpx("v", v("fd", C, 640), v("f", 1024, 1344), v("ld"))
 
     def pre_b1():
         cpx("s", v("qa", 640, 960), v("f", 0, C), v("lu", 0, Q))
@@ -259,10 +271,8 @@ def rank_program(g, core, T, topo):
         scan(v("qas", 0, 640), v("mf"), v("qa", 0, 640))
         if then:
             then()
-        raw = v("qas", 15, 1280, 16)
-        ts(v("ix"), raw, corr, A.subtract, 319.5, A.is_gt)
-        ts(v("ae"), raw, corr, A.subtract, 320.0, A.is_lt)
-        ts(v("ix"), v("ix"), 320.0, A.mult)
+        ts(v("ix"), v("qas", 15, 1280, 16), pc[4], A.is_gt, 320.0, A.mult)
+        act(v("ae"), v("ix"), F.Copy, -0.003125, 1.0)
         tt(v("lx"), v("ix"), v("ei"), A.add)
 
     def pre_c2():
@@ -284,24 +294,41 @@ def rank_program(g, core, T, topo):
         tt(v("dp", 0, 40), v("r", 0, 40), v("sw", 0, 40), A.add)
         tt(v("p0", 60, 80), v("p0", 40, 60), v("a512"), A.add)
 
-    tables("wu0", "ssv")
+    tables("wu0")
     pre_a()
-    pre_b0()
-    ts(v("ma"), v("row"), pc[0], A.is_gt)
-    act(v("mf"), v("ma"), F.Copy, 67584.0, -65536.0)
     quant(v("uq"), v("us"), v("ut"))
     cp(v("ul"), v("ui"))
     op("v", lambda: g.vector.tensor_copy(T.pq[:, 0:256].bitcast(dt.uint32), T.uq[:, 0:128].bitcast(dt.uint32).indirect(T.ul[:, 0:16])), [v("uq"), v("ul")], [v("pq")])
     pre_a2()
+    pre_b0("v")
+    act(v("mb", 0, C), v("ma"), F.Copy, 66.0, -64.0)
+    spread("mb", (1, 2, 3))
     pre_b1()
     op("s", lambda: g.scalar.activation(T.pz[:, 0:256], T.us[:, 0:128].indirect(T.ul[:, 0:16]), F.Copy), [v("us"), v("ul")], [v("pz")])
     pre_b2()
-    act(v("mb", 0, 640), v("ma"), F.Copy, 66.0, -64.0)
-    op("y", lambda: g.sync.dma_start(T.mb[:, 640:1280], T.mb[:, 0:640]), [v("mb", 0, 640)], [v("mb", 640, 1280)])
-    quant(v("xq"), v("xs"), v("xi"))
+
+    half = [(0, C // 2), (C // 2, C)]
+
+    def part(k):
+        return v("ps", 512 * k, 512 * k + C // 2)
+
+    def scores(h):
+        c, d = half[h]
+        quant(v("xq", c, d), v("xs", c, d), v("xi", 4 * c, 4 * d))
+        for i in range(2):
+            mm(part(4 + 2 * h + i), v("pq", 128 * i, 128 * i + 128), v("pz", 128 * i, 128 * i + 128), v("xq", c, d), v("xs", c, d))
+
+    for h in range(2):
+        scores(h)
+
+    def signs(h):
+        c, d = half[h]
+        act(v("sa", c, d), part(4 + 2 * h), F.Sign, 1.0, -2.0 ** -93)
+        act(v("nb", C + c, C + d), part(5 + 2 * h), F.Sign)
 
     def differ():
-        ts(v("ab"), v("sa"), -0.5, A.mult)
+        for c, d in half:
+            ts(v("ab", c, d), v("sa", c, d), -0.5, A.mult)
         ttx(v("nb", 0, C), v("ab"), v("ld"), v("sa"), A.mult)
 
     for r in range(3):
@@ -309,22 +336,22 @@ def rank_program(g, core, T, topo):
         to = T.cores[rank ^ STEP[r]]
         ins = len(topo.engines(to, core))
         wu, la = "wu%d" % (r + 1), v("la%d" % r)
-        mm(bank(0), v("pq", 0, 128), v("pz", 0, 128), v("xq"), v("xs"))
-        mm(bank(1), v("pq", 128, 256), v("pz", 128, 256), v("xq"), v("xs"))
-        act(v("sa"), bank(0), F.Sign, 1.0, -2.0 ** -93)
-        act(v("nb", C, 640), bank(1), F.Sign)
+        for h in range(2):
+            signs(h)
         if r == 0:
             pre_c1(differ)
         else:
             pre_c3()
             differ()
         cpx("s", v("bf", 0, 640), v("nb"), v("lx", 0, 40))
-        cpx("s", v("bf", 960, 1280), v("nb"), v("lx", 60, 80))
         if r == 0:
-            for b in range(4):
-                halve(b)
+            cpx("s", v("bf", 640, 960), v("nb"), v("lx", 40, 60))
+        cpx("s", v("bf", 960, 1280), v("nb"), v("lx", 60, 80))
+        for b in range(4):
+            halve(b)
         scan(v("nbs"), v("mb", 0, 640), v("nb"))
-        cpx("v", v("bf", 640, 960), v("nb"), v("lx", 40, 60))
+        if r:
+            cpx("v", v("bf", 640, 960), v("nb"), v("lx", 40, 60))
         ts(v("n2"), v("nbs", 15, 640, 16), thr, A.is_ge)
         tt(v("tb"), v("n2", Q, 40), inact, A.mult)
         tt(v("sv", Q, 40), v("n2", 0, Q), inact, A.add)
@@ -368,13 +395,14 @@ def rank_program(g, core, T, topo):
         ts(v("mi"), v("mgs", 15, C, 16), corr, A.subtract)
         ts(v("mj"), v("mi"), 511, A.bitwise_and)
         cp(v("mu"), v("mj"))
-        for t in (0, 3, 1, 2):
-            cpx("s" if t < 2 else "v", v("ht", t, 1280, 4), hp[t], v("mu"))
-        hq, hs, aq, az = (v(n + "%d" % r) for n in ("hq", "hs", "aq", "as"))
-        quant(hq, hs, v("ht"))
-        send(to, aq, hq, "ah%d" % r, True)
-        send(to, az, hs, "ah%d" % r)
-        op("x", None, [], [aq, az], sem=("ah%d" % r, 2 * ins))
+        for h, (c, d) in enumerate(half if last else [(0, C)]):
+            for t in (0, 3, 1, 2):
+                cpx("s" if t < 2 else "v", v("ht", 4 * c + t, 4 * d, 4), hp[t], v("mu", c // 16, d // 16))
+            hq, hs, aq, az = (v(n + "%d" % r, c, d) for n in ("hq", "hs", "aq", "as"))
+            quant(hq, hs, v("ht", 4 * c, 4 * d))
+            send(to, aq, hq, "ah%d" % (r + h), True)
+            send(to, az, hs, "ah%d" % (r + h))
+            op("x", None, [], [aq, az], sem=("ah%d" % (r + h), 2 * ins))
         if last:
             cpx("s", v("fo", 0, C), v("ioo"), v(wu, 40, 60))
             cpx("s", v("fo", C, 960), v("ioo"), v(wu, 0, 40))
@@ -389,21 +417,27 @@ def rank_program(g, core, T, topo):
                 quant(v("eq"), v("es"), v("et"))
             pre_c1()
             pre_c2()
-        for b in range(4):
-            k = (128 * b, 128 * b + 128)
-            mm(bank(4 + b), v("eq", *k), v("es", *k), aq, az)
-        for b in range(4):
-            x = v("xi", b, 1280, 4)
-            tt(x, bank(4 + b), x, A.add)
+        for h, (c, d) in enumerate(half):
+            for b in range(4):
+                k = (128 * b, 128 * b + 128)
+                mm(part(4 - 4 * h + b), v("eq", *k), v("es", *k), v("aq%d" % r, c, d), v("as%d" % r, c, d))
+        for h, (c, d) in enumerate(half):
+            for b in range(4):
+                x = v("xi", 4 * c + b, 4 * d, 4)
+                tt(x, part(4 - 4 * h + b), x, A.add)
             if not last:
-                halve(b)
-        quant(v("xq"), v("xs"), v("xi"))
-    op("y", lambda: g.sync.dma_start(T.oc[:], T.xq[:].bitcast(dt.uint8)), [v("xq")], [])
+                scores(h)
+                continue
+            quant(v("xq", c, d), v("xs", c, d), v("xi", 4 * c, 4 * d))
+            mm(part(4 + h), v("vq"), v("vs"), v("xq", c, d), v("xs", c, d))
+            op("y", lambda c=c, d=d: g.sync.dma_start(T.oc[:, 4 * c:4 * d], T.xq[:, c:d].bitcast(dt.uint8)), [v("xq", c, d)], [])
+            if h == 0:
+                act(v("yo", c, d), part(4), F.Copy)
+            else:
+                cp(v("yo", c, d), part(5))
+            op("yd"[1 - h], lambda c=c, d=d, e=(g.sync if h else g.scalar): e.dma_start(T.y[:, c:d], T.yo[:, c:d]), [v("yo", c, d)], [])
     for k in range(4):
-        op("y" if k % 2 else "d", lambda k=k: (g.sync if k % 2 else g.scalar).dma_start(T.osc[4 * k:4 * k + 4, :], T.xs[32 * k:32 * k + 4, :]), [v("xs")], [])
-    mm(bank(2), v("vq"), v("vs"), v("xq"), v("xs"))
-    cp(v("yo"), bank(2))
-    op("y", lambda: g.sync.dma_start(T.y[:], T.yo[:]), [v("yo")], [])
+        op("d", lambda k=k: g.scalar.dma_start(T.osc[4 * k:4 * k + 4, :], T.xs[32 * k:32 * k + 4, :]), [v("xs")], [])
 
     emit()
-    g.wait_ge(T.sem["loc"], sum(3 * len(topo.engines(core, T.cores[rank ^ s])) for s in STEP))
+    g.wait_ge(T.sem["loc"], sum((5 if s == STEP[-1] else 3) * len(topo.engines(core, T.cores[rank ^ s])) for s in STEP))

from concourse.mybir import dt, AluOpType as A, ActivationFunctionType as F

N, C, Q, P = 8, 320, 20, 512
STEP = [1, 2, 4]
X4, U8, BF, FP, IN, US = "float8_e4m3fn_x4", "uint8", "bfloat16", "float32", "int32", "uint16"
SCRATCH = {"ps": ("psum", [128, 4096], FP)}
for _t, _l in (
        (X4, "uq 128 pq 256 vq 128 wq 512 eq 512 xq 320 zq 320"),
        (U8, "us 128 pz 256 vs 128 wp 512 es 512 xs 320 zs 320"),
        (BF, "xi 1280 xh 1280 ut 512 vt 512 eo 512 et 2048 gt 1280 zt 1280 hp 1280 ht 1280"),
        (BF, "row 320 ma 320 mb 1280 mf 640 ab 320 sa 320 nb 640 nbs 640 bf 1280 bfs 1280"),
        (IN, "wi 60 pid 1 pim 1 ui 16 li 40 mi 20 mj 20 tt 100 ei 80"),
        (US, "ul 16 ld 20 ldx 20 eu 80 lx 80 lu 40 mu 20"),
        (FP, "pc 5 io_ 1536 ioo 1536 cr 20 cw 20 b1 60 b2 60 f 1536 fo 960 fd 640 fds 640 qa 1280 qas 1280 mg 320 mgs 320 yo 320"),
        (FP, "act 20 inn 20 tb 20 t0 20 t1 20 t4 20 inw 20 actd 20 a512 20 kk 80 c1 80 hh 80 sw 80 g1 80 ae 80 r 80"),
        (FP, "pa 80 ix 80 dp 120 p0 120 n2 40 sv 60 bt 80 m 120 a5 120 d2 60")):
    _l = _l.split()
    for _i in range(0, len(_l), 2):
        SCRATCH[_l[_i]] = ("sbuf", [128, int(_l[_i + 1])], _t)
for _r in range(4):
    SCRATCH["wu%d" % _r] = ("sbuf", [128, 60], US)
for _r in range(3):
    for _n, _w, _t in (("la", Q, US), ("hq", C, X4), ("hs", C, U8), ("aq", C, X4), ("as", C, U8)):
        SCRATCH["%s%d" % (_n, _r)] = ("sbuf", [128, _w], _t)
POOL = {"v": 44, "s": 24, "t": 20, "g": 14, "y": 20, "d": 8}
SEMAPHORES = ["%s%d" % (q, i) for q in POOL for i in range(POOL[q])] + ["loc"] + ["al%d" % i for i in range(3)] + ["ah%d" % i for i in range(4)]


def recorder(g, T):
    ops, hist, maps = [], {}, {}
    queue = {"v": g.vector, "s": g.scalar, "t": g.tensor, "g": g, "y": g.sync, "d": g.scalar}

    def cols(v):
        name, a, b, s = v
        if SCRATCH[name][0] == "psum":
            a, b, s = a // 512, (b + 511) // 512, 1
        k = (a, b, s)
        if k not in maps:
            maps[k] = sum(1 << i for i in range(a, b, s))
        return maps[k]

    def op(q, fn, rd, wr, sem=None):
        me, deps = len(ops), set()
        eng = "s" if q == "d" else q
        for lst, w in ((rd, False), (wr, True)):
            for v in lst:
                m, psum = cols(v), SCRATCH[v[0]][0] == "psum"
                for o, om, ow, oe in hist.setdefault(v[0], []):
                    if om & m and (w or ow or (psum and oe != eng)):
                        deps.add(o)
        for lst, w in ((rd, False), (wr, True)):
            for v in lst:
                m, h = cols(v), hist[v[0]]
                if w:
                    h[:] = [x for x in h if x[1] & ~m or x[0] == me]
                h.append((me, m, w, eng))
        deps.discard(me)
        ops.append({"q": q, "eng": eng, "fn": fn, "deps": deps, "sem": sem, "waits": [], "inc": False})

    def emit():
        known, at = {}, []
        for o in ops:
            k = known.get(o["eng"], 0)
            for d in sorted(o["deps"], reverse=True):
                if not k >> d & 1:
                    o["waits"].append(d)
                    ops[d]["inc"] = True
                    k |= 1 << d | at[d]
            at.append(k)
            known[o["eng"]] = k
        pool, total = {}, {}
        for i, o in enumerate(ops):
            if o["fn"] is None:
                total[o["sem"][0]] = o["sem"][1]
                o["at"] = o["sem"]
                continue
            dma = o["q"] in "yd"
            if o["sem"] is None and (o["inc"] or dma):
                p = pool.setdefault(o["q"], [])
                for s in p:
                    if at[i] >> s[1] & 1:
                        break
                else:
                    s = ["%s%d" % (o["q"], len(p)), 0]
                    p.append(s)
                s[1] = i
                total[s[0]] = total.get(s[0], 0) + (16 if dma else 1)
                o["at"] = (s[0], total[s[0]])
            qu = queue[o["q"]]
            for d in sorted(o["waits"]):
                qu.wait_ge(T.sem[ops[d]["at"][0]], ops[d]["at"][1])
            ins = o["fn"]()
            if "at" in o:
                ins.then_inc(T.sem[o["at"][0]], 16 if dma else 1)
        for s in sorted(total):
            g.wait_ge(T.sem[s], total[s])

    return op, emit


def rank_program(g, core, T, topo):
    rank = T.rank_of(core)
    if rank is None:
        return
    op, emit = recorder(g, T)

    def v(name, a=0, b=None, s=1):
        return (name, a, SCRATCH[name][1][1] if b is None else b, s)

    def ap(w):
        n, a, b, s = w
        return T[n][:, a:b] if s == 1 else T[n][:, a:b:s]

    def by(win, off):
        return ap(win).indirect(ap(off))

    def tt(out, a, b, o):
        op("v", lambda: g.vector.tensor_tensor(ap(out), ap(a), ap(b), o), [a, b], [out])

    def ttx(out, win, off, b, o):
        op("v", lambda: g.vector.tensor_tensor(ap(out), by(win, off), ap(b), o), [win, off, b], [out])

    def ts(out, a, s1, o1, s2=None, o2=None):
        rd = [a] + [s for s in (s1, s2) if isinstance(s, tuple)]
        k1, k2 = (ap(s) if isinstance(s, tuple) else s for s in (s1, s2))
        if o2 is None:
            op("v", lambda: g.vector.tensor_scalar(ap(out), ap(a), k1, None, o1), rd, [out])
        else:
            op("v", lambda: g.vector.tensor_scalar(ap(out), ap(a), k1, k2, o1, o2), rd, [out])

    def cp(out, a):
        op("v", lambda: g.vector.tensor_copy(ap(out), ap(a)), [a], [out])

    def cpx(q, out, win, off):
        if q == "v":
            op("v", lambda: g.vector.tensor_copy(ap(out), by(win, off)), [win, off], [out])
        else:
            op("s", lambda: g.scalar.activation(ap(out), by(win, off), F.Copy), [win, off], [out])

    def act(out, a, fn, scale=1.0, bias=0.0):
        if isinstance(bias, tuple):
            op("s", lambda: g.scalar.activation(ap(out), ap(a), fn, bias=ap(bias), scale=scale), [a, bias], [out])
        else:
            op("s", lambda: g.scalar.activation(ap(out), ap(a), fn, bias=bias, scale=scale), [a], [out])

    def scan(out, m, a):
        op("v", lambda: g.vector.tensor_tensor_scan(ap(out), ap(m), ap(a), 0.0, A.add, A.max), [m, a], [out])

    def quant(q, s, t):
        op("v", lambda: g.vector.quantize_mx(ap(q), ap(s), ap(t)), [t], [q, s])

    def mm(out, w, ws, x, xs):
        op("t", lambda: g.tensor.matmul_mx(ap(out), ap(w), ap(ws), ap(x), ap(xs), True, True), [w, ws, x, xs], [out])

    def iota(out, pat, base, cm, small=False):
        if small:
            op("g", lambda: g.iota(ap(out), pat, base, cm, allow_small_or_imprecise_dtypes=True), [], [out])
        else:
            op("g", lambda: g.iota(ap(out), pat, base, cm), [], [out])

    def load(q, out, src, codes=False):
        e = g.sync if q == "y" else g.scalar
        o = T[out][:].bitcast(dt.uint8) if codes else T[out][:]
        op(q, lambda: e.dma_start(o, src[:]), [], [v(out)])

    def bank(k):
        return v("ps", 512 * k, 512 * k + C)

    def send(to, dst, src, sem, codes=False):
        rid, pid, _ = topo.addr(to)
        o, i = (ap(dst).bitcast(dt.uint8), ap(src).bitcast(dt.uint8)) if codes else (ap(dst), ap(src))
        op("g", lambda: g.remote_dma(o, i, T.sem[sem], T.sem["loc"], pid, rid, topo.mask(core, to)), [src], [], sem=("", 0))

    op("y", lambda: g.sync.dma_start(T.wi[:, 0:40], T.wl[:, Q:60]), [], [v("wi", 0, 40)])
    op("d", lambda: g.scalar.dma_start(T.wi[:, 40:60], T.wl[:, 0:Q]), [], [v("wi", 40, 60)])
    load("y", "xi", T.x)
    load("d", "ut", T.u)
    load("y", "wp", T.ws)
    load("y", "wq", T.wc, True)
    load("d", "vt", T.v)

    iota(v("pid"), [[0, 1]], 0, 1)
    iota(v("cr"), [[16, Q]], 0, 0, True)
    iota(v("io_", 0, C), [[1, C]], 0, 0, True)
    iota(v("row"), [[0, 20], [1, 16]], 0, 0, True)
    iota(v("ui"), [[1, 2], [16, 8]], 0, 0)
    op("v", lambda: g.vector.memset(T.eo[:], 1.0), [], [v("eo")])
    for k in range(2):
        for n in ("io_", "f"):
            o = v(n, P * k + C, P * k + P)
            op("v", lambda o=o: g.vector.memset(ap(o), 0.0), [], [o])
    for b in range(4):
        o = v("et", 512 * b, 512 * b + 512)
        op("g", lambda o=o, b=b: g.affine_select(ap(o), T.eo[:], [[1, 512]], A.is_equal, 0.0, -b, -4), [v("eo")], [o])
    iota(v("ioo"), [[C, 3], [1, P]], 0, 0, True)
    ts(v("pim"), v("pid"), 15, A.bitwise_and)
    pc = [v("pc", i, i + 1) for i in range(5)]
    cp(pc[0], v("pim"))
    thr, corr = pc[1], pc[2]
    ts(thr, pc[0], -2.0, A.mult, 30.25, A.add)
    ts(corr, pc[0], -2048.0, A.mult, 30720.0, A.add)
    ts(pc[3], pc[0], 2048.0, A.mult, -31744.0, A.add)
    ts(pc[4], pc[0], -2048.0, A.mult, 31136.0, A.add)
    ts(v("cw"), v("cr"), pc[0], A.add)
    for k in (1, 2):
        act(v("io_", P * k, P * k + C), v("io_", 0, C), F.Copy, 1.0, 1.0 * P * k)
    ts(v("ma"), v("row"), pc[0], A.is_gt)

    def spread(n, ks):
        for k in ks:
            op("y", lambda k=k: g.sync.dma_start(T[n][:, C * k:C * k + C], T[n][:, 0:C]), [v(n, 0, C)], [v(n, C * k, C * k + C)])

    act(v("mf", 0, C), v("ma"), F.Copy, 67584.0, -65536.0)
    spread("mf", (1,))
    ts(v("b1"), v("wi"), 320.0, A.is_ge, 192.0, A.mult)
    ts(v("b2"), v("wi"), 640.0, A.is_ge, 192.0, A.mult)
    tt(v("b1"), v("b1"), v("b2"), A.add)
    new, w1, w2, w0, t80 = v("tt", 40, 100), v("tt", 40, 60), v("tt", 60, 80), v("tt", 80, 100), v("tt", 0, 80)
    tt(v("wu0"), v("wi"), v("b1"), A.add)
    tt(new, v("wi"), v("b1"), A.add)
    ts(v("li"), v("tt", 40, 80), 511, A.bitwise_and)
    cp(v("lu"), v("li"))

    def halve(b):
        act(v("xh", C * b, C * b + C), v("xi", b, 1280, 4), F.Copy, 0.5)

    def tables(wu, qs="sss"):
        for k in range(3):
            j = (40, 0, Q)[k]
            cpx(qs[k], v("f", P * k, P * k + C), v("io_", 0, 1344), v(wu, j, j + Q))

    inact = v("inn")

    def pre_a():
        ts(v("act"), w0, 320.0, A.is_lt)
        ts(inact, w0, 320.0, A.is_ge)
        tt(v("actd"), v("act"), w0, A.mult)
        tt(v("t0"), inact, v("cw"), A.mult)
        ts(v("a512"), w0, 320.0, A.is_lt, 512.0, A.mult)
        tt(v("ld"), v("actd"), v("t0"), A.add)
        tt(v("t1"), v("t0"), v("a512"), A.add)
        tt(v("ldx"), v("actd"), v("t1"), A.add)

    def pre_a2():
        tt(v("t4"), v("act"), w2, A.mult)
        tt(v("inw"), w0, v("actd"), A.subtract)
        tt(w2, v("t4"), v("inw"), A.add)

    def pre_b0(q="s"):
        cpx(q, v("fd", C, 640), v("f", 1024, 1344), v("ld"))
        cpx("s", v("fd", 0, C), v("f", 0, 1344), v("ldx"))

    def pre_b1():
        cpx("s", v("qa", 640, 960), v("f", 0, C), v("lu", 0, Q))

    def pre_b2():
        scan(v("fds"), v("mf"), v("fd"))
        ts(v("tt", 0, 40), v("fds", 15, 640, 16), corr, A.subtract)
        ts(v("ei"), t80, 511, A.bitwise_and)
        cp(v("eu"), v("ei"))
        cpx("s", v("qa", 0, 640), v("f", 0, C), v("eu", 0, 40))
        cpx("v", v("qa", 960, 1280), v("f", 0, C), v("eu", 60, 80))
        tt(v("kk"), t80, v("ei"), A.subtract)

    def pre_c1(then=None):
        act(v("hh"), v("kk"), F.Identity, 2.0, pc[3])
        act(v("g1"), v("kk"), F.Copy, -3.0, 2048.0)
        act(v("sw"), v("kk"), F.Abs, 2.0, -1280.0)
        act(v("sw"), v("sw"), F.Copy, 1.0, -768.0)
        scan(v("qas", 640, 1280), v("mf"), v("qa", 640, 1280))
        scan(v("qas", 0, 640), v("mf"), v("qa", 0, 640))
        if then:
            then()
        ts(v("ix"), v("qas", 15, 1280, 16), pc[4], A.is_gt, 320.0, A.mult)
        act(v("ae"), v("ix"), F.Copy, -0.003125, 1.0)
        tt(v("lx"), v("ix"), v("ei"), A.add)

    def pre_c2():
        tt(v("c1"), v("hh"), v("ei"), A.subtract)
        tt(v("pa"), v("ae"), v("g1"), A.mult)
        tt(v("r"), v("qas", 15, 1280, 16), v("c1"), A.add)
        tt(v("p0", 80, 120), v("pa", 40, 80), v("tt", 40, 80), A.add)
        tt(v("r"), v("r"), v("ae"), A.mult)
        tt(v("p0", 0, 40), v("pa", 0, 40), v("tt", 0, 40), A.add)
        tt(v("p0", 40, 60), v("p0", 80, 100), inact, A.mult)

    def pre_c3():
        tt(v("dp", 80, 120), v("r", 40, 80), v("sw", 40, 80), A.add)
        tt(v("p0", 40, 60), v("p0", 40, 60), v("actd"), A.add)
        tt(v("dp", 60, 80), v("dp", 80, 100), inact, A.mult)
        tt(v("dp", 40, 60), v("dp", 80, 100), inact, A.mult)

    def pre_c4():
        tt(v("dp", 0, 40), v("r", 0, 40), v("sw", 0, 40), A.add)
        tt(v("p0", 60, 80), v("p0", 40, 60), v("a512"), A.add)

    tables("wu0")
    pre_a()
    quant(v("uq"), v("us"), v("ut"))
    cp(v("ul"), v("ui"))
    op("v", lambda: g.vector.tensor_copy(T.pq[:, 0:256].bitcast(dt.uint32), T.uq[:, 0:128].bitcast(dt.uint32).indirect(T.ul[:, 0:16])), [v("uq"), v("ul")], [v("pq")])
    pre_a2()
    pre_b0("v")
    act(v("mb", 0, C), v("ma"), F.Copy, 66.0, -64.0)
    spread("mb", (1, 2, 3))
    pre_b1()
    op("s", lambda: g.scalar.activation(T.pz[:, 0:256], T.us[:, 0:128].indirect(T.ul[:, 0:16]), F.Copy), [v("us"), v("ul")], [v("pz")])
    pre_b2()

    half = [(0, C // 2), (C // 2, C)]

    def part(k):
        return v("ps", 512 * k, 512 * k + C // 2)

    def scores(h):
        c, d = half[h]
        quant(v("xq", c, d), v("xs", c, d), v("xi", 4 * c, 4 * d))
        for i in range(2):
            mm(part(4 + 2 * h + i), v("pq", 128 * i, 128 * i + 128), v("pz", 128 * i, 128 * i + 128), v("xq", c, d), v("xs", c, d))

    for h in range(2):
        scores(h)

    def signs(h):
        c, d = half[h]
        act(v("sa", c, d), part(4 + 2 * h), F.Sign, 1.0, -2.0 ** -93)
        act(v("nb", C + c, C + d), part(5 + 2 * h), F.Sign)

    def differ():
        for c, d in half:
            ts(v("ab", c, d), v("sa", c, d), -0.5, A.mult)
        ttx(v("nb", 0, C), v("ab"), v("ld"), v("sa"), A.mult)

    for r in range(3):
        last = r == 2
        to = T.cores[rank ^ STEP[r]]
        ins = len(topo.engines(to, core))
        wu, la = "wu%d" % (r + 1), v("la%d" % r)
        for h in range(2):
            signs(h)
        if r == 0:
            pre_c1(differ)
        else:
            pre_c3()
            differ()
        cpx("s", v("bf", 0, 640), v("nb"), v("lx", 0, 40))
        if r == 0:
            cpx("s", v("bf", 640, 960), v("nb"), v("lx", 40, 60))
        cpx("s", v("bf", 960, 1280), v("nb"), v("lx", 60, 80))
        for b in range(4):
            halve(b)
        scan(v("nbs"), v("mb", 0, 640), v("nb"))
        if r:
            cpx("v", v("bf", 640, 960), v("nb"), v("lx", 40, 60))
        ts(v("n2"), v("nbs", 15, 640, 16), thr, A.is_ge)
        tt(v("tb"), v("n2", Q, 40), inact, A.mult)
        tt(v("sv", Q, 40), v("n2", 0, Q), inact, A.add)
        tt(v("sv", 0, Q), v("n2", 0, Q), v("tb"), A.add)
        tt(v("sv", 40, 60), v("n2", 0, Q), v("tb"), A.add)
        if r == 0:
            pre_c2()
            pre_c3()
        pre_c4()
        scan(v("bfs", 0, 960), v("mb", 0, 960), v("bf", 0, 960))
        scan(v("bfs", 960, 1280), v("mb", 0, C), v("bf", 960, 1280))
        ts(v("bt"), v("bfs", 15, 1280, 16), thr, A.is_ge)
        tt(v("m", 0, 60), v("bt", 0, 60), v("dp", 0, 60), A.mult)
        tt(v("m", 60, 80), v("bt", 40, 60), v("dp", 60, 80), A.mult)
        tt(v("m", 80, 120), v("bt", 40, 80), v("dp", 80, 120), A.mult)
        tt(v("a5"), v("m"), v("p0"), A.add)
        tt(v("d2"), v("a5", 0, 60), v("a5", 60, 120), A.subtract)
        tt(v("d2"), v("d2"), v("sv"), A.mult)
        tt(new, v("d2"), v("a5", 60, 120), A.add)
        ts(v("li"), v("tt", 40, 80), 511, A.bitwise_and)
        cp(v("lu"), v("li"))
        cp(v(wu), new)
        send(to, la, v(wu, 40, 60), "al%d" % r)
        op("x", None, [], [la], sem=("al%d" % r, ins))
        for t in range(4):
            cpx("sssv"[t], v("gt", C * t, C * t + C), v("xh", C * t, C * t + C), v("lu", 0, Q))
        for t in range(4):
            ttx(v("zt", t, 1280, 4), v("xh", C * t, C * t + C), v("lu", Q, 40), v("gt", C * t, C * t + C), A.add)
        quant(v("zq"), v("zs"), v("zt"))
        for b in range(4):
            k = (128 * b, 128 * b + 128)
            mm(bank(b), v("wq", *k), v("wp", *k), v("zq"), v("zs"))
        tables(wu)
        if not last:
            pre_a()
        hp = [v("hp", C * b, C * b + C) for b in range(4)]
        cpx("v", v("mg"), v("f", 0, 1344), la)
        for b in range(4):
            act(hp[b], bank(b), F.Copy, 0.03125)
        scan(v("mgs"), v("mf", 0, C), v("mg"))
        ts(v("mi"), v("mgs", 15, C, 16), corr, A.subtract)
        ts(v("mj"), v("mi"), 511, A.bitwise_and)
        cp(v("mu"), v("mj"))
        for h, (c, d) in enumerate(half if last else [(0, C)]):
            for t in (0, 3, 1, 2):
                cpx("s" if t < 2 else "v", v("ht", 4 * c + t, 4 * d, 4), hp[t], v("mu", c // 16, d // 16))
            hq, hs, aq, az = (v(n + "%d" % r, c, d) for n in ("hq", "hs", "aq", "as"))
            quant(hq, hs, v("ht", 4 * c, 4 * d))
            send(to, aq, hq, "ah%d" % (r + h), True)
            send(to, az, hs, "ah%d" % (r + h))
            op("x", None, [], [aq, az], sem=("ah%d" % (r + h), 2 * ins))
        if last:
            cpx("s", v("fo", 0, C), v("ioo"), v(wu, 40, 60))
            cpx("s", v("fo", C, 960), v("ioo"), v(wu, 0, 40))
            op("y", lambda: g.sync.dma_start(T.ow[:], T.fo[0:128:16, 0:960]), [v("fo")], [])
            quant(v("vq"), v("vs"), v("vt"))
        else:
            pre_b0()
            pre_a2()
            pre_b1()
            pre_b2()
            if r == 0:
                quant(v("eq"), v("es"), v("et"))
            pre_c1()
            pre_c2()
        for h, (c, d) in enumerate(half):
            for b in range(4):
                k = (128 * b, 128 * b + 128)
                mm(part(4 - 4 * h + b), v("eq", *k), v("es", *k), v("aq%d" % r, c, d), v("as%d" % r, c, d))
        for h, (c, d) in enumerate(half):
            for b in range(4):
                x = v("xi", 4 * c + b, 4 * d, 4)
                tt(x, part(4 - 4 * h + b), x, A.add)
            if not last:
                scores(h)
                continue
            quant(v("xq", c, d), v("xs", c, d), v("xi", 4 * c, 4 * d))
            mm(part(4 + h), v("vq"), v("vs"), v("xq", c, d), v("xs", c, d))
            op("y", lambda c=c, d=d: g.sync.dma_start(T.oc[:, 4 * c:4 * d], T.xq[:, c:d].bitcast(dt.uint8)), [v("xq", c, d)], [])
            if h == 0:
                act(v("yo", c, d), part(4), F.Copy)
            else:
                cp(v("yo", c, d), part(5))
            op("yd"[1 - h], lambda c=c, d=d, e=(g.sync if h else g.scalar): e.dma_start(T.y[:, c:d], T.yo[:, c:d]), [v("yo", c, d)], [])
    for k in range(4):
        op("d", lambda k=k: g.scalar.dma_start(T.osc[4 * k:4 * k + 4, :], T.xs[32 * k:32 * k + 4, :]), [v("xs")], [])

    emit()
    g.wait_ge(T.sem["loc"], sum((5 if s == STEP[-1] else 3) * len(topo.engines(core, T.cores[rank ^ s])) for s in STEP))
